import numpy as np, ml_dtypes
CORES = [8,136,40,168]
N = 4
BF = ml_dtypes.bfloat16
def gentries(a):
    return np.ascontiguousarray(a.reshape(8, 16, -1).transpose(0, 2, 1)).reshape(8, -1)
def gtable(e):
    e = np.asarray(e); return np.ascontiguousarray(e.reshape(8, -1, 16).transpose(0, 2, 1)).reshape(128, -1).astype(np.int32)
I, W, PL, RO, CNT, B, AS = 192, 3072, 1024, 6, 11, 48, 64
def records(x, s):
    return np.take_along_axis(x, s.transpose(0, 1, 3, 2).reshape(N, 8, 1, 16 * I), 3).reshape(N, 8, 16, I, 16)
def dist(xs, z):
    return np.sum(np.abs(xs - z[..., None]), axis=2).transpose(0, 1, 3, 2)
def parts(rng):
    x = (256 * rng.random((N, 8, 16, W)) * rng.choice(np.array([1.0, 1.0, 0.5, 0.25]), (N, 8, 1, W))).astype(np.int64)
    z = rng.integers(0, 256, (N, 8, 16, I)); f = rng.integers(0, 256, (N, 8, 16, I))
    s = rng.integers(0, W, (N, 8, 16, I)); pl = rng.integers(0, W, (N, 8, 16, PL)); p = rng.integers(0, PL, (N, 8, I))
    th = rng.integers(300, 1300, (N, 8, 1, I)) + rng.integers(0, 200, (N, 8, 16, I))
    return x, z, f, s, pl, p, th
def pack(x, z, f, s, pl, p, th):
    return {"x0": x.reshape(N, 128, W).astype(np.float32).astype(BF), "z0": z.reshape(N, 128, I).astype(np.float32).astype(BF), "f0": f.reshape(N, 128, I).astype(np.float32).astype(BF),
            "s0": s.reshape(N, 128, I).astype(np.int32), "pl": pl.reshape(N, 128, PL).astype(np.int32), "p0": np.stack([gtable(a) for a in p]), "th": th.reshape(N, 128, I).astype(np.int32)}
def setup_inputs(rng):
    return pack(*parts(rng))
def setup_inputs_spread(rng):
    x = (np.exp2(8 * rng.random((N, 8, 1, W))) * rng.random((N, 8, 16, W))).astype(np.int64)
    z = (np.exp2(8 * rng.random((N, 8, 1, I))) * rng.random((N, 8, 16, I))).astype(np.int64)
    f = (np.exp2(8 * rng.random((N, 8, 1, I))) * rng.random((N, 8, 16, I))).astype(np.int64)
    s = (W * rng.random((N, 8, 16, I)) ** 3).astype(np.int64); pl = (W * rng.random((N, 8, 16, PL)) ** 2).astype(np.int64); p = (PL * rng.random((N, 8, I)) ** 3).astype(np.int64)
    th = np.minimum((np.exp2(5 + 7 * rng.random((N, 8, 1, I))) * (0.5 + 0.5 * rng.random((N, 8, 16, I)))).astype(np.int64), 4080)
    return pack(np.minimum(x, 255), np.minimum(z, 255), np.minimum(f, 255), np.minimum(s, W - 1), np.minimum(pl, W - 1), np.minimum(p, PL - 1), th)
def setup_inputs_ends(rng):
    def mix(n):
        return np.where(rng.random((N, 8, 1, n)) < 0.5, rng.integers(0, 2, (N, 8, 16, n)), rng.integers(0, 2, (N, 8, 1, n)))
    x = 255 * mix(W); z = 255 * mix(I); f = 255 * mix(I); th = 4080 * mix(I)
    s = (W - 1) * rng.integers(0, 2, (N, 8, 16, I)); pl = (W - 1) * rng.integers(0, 2, (N, 8, 16, PL)); p = (PL - 1) * rng.integers(0, 2, (N, 8, I))
    x[:, 1::2, :, W - 1] = 255; x[:, 1::2, :, 0] = 0; x[:, 0:4:2, :, W - 1] = 0; x[:, 0:4:2, :, 0] = 255
    pl[:, 7, :, PL - 1] = W - 1; pl[:, 7, :, 0] = 0; pl[:, 7, 0, 768] = 0
    for i in (0, 1, I - 2, I - 1):
        z[:, 7, :, i] = 0; f[:, 7, :, i] = 0; s[:, 7, :, i] = W - 1; th[:, 7, :, i] = 4080; p[:, 7, i] = PL - 1
    for i in (2, 3, I - 4, I - 3):
        z[:, 7, :, i] = 255; f[:, 7, :, i] = 255; s[:, 7, :, i] = 0; th[:, 7, :, i] = 4080; p[:, 7, i] = 0
    return pack(x, z, f, s, pl, p, th)
def setup_inputs_ties(rng):
    x, z, f, s, pl, p, th = parts(rng)
    x = 64 * rng.integers(0, 4, (N, 8, 16, W)); z = 64 * rng.integers(0, 4, (N, 8, 16, I))
    few = np.take_along_axis(rng.integers(0, W, (N, 8, 3, I)), rng.integers(0, 3, (N, 8, 16, I)), 2)
    s = np.where(rng.random((N, 8, 1, I)) < 0.5, few, s)
    ds = dist(records(x, s), z); dp = dist(records(x, np.take_along_axis(pl, p[:, :, None, :], 3)), z)
    one = (rng.random((N, 8, 16, I)) < 0.08).astype(np.int64); k = rng.integers(0, 3, (N, 8, 1, I))
    th = np.where(k == 0, ds + one, np.where(k == 1, np.minimum(dp + one, ds), np.minimum(dp, ds)))
    return pack(x, z, f, s, pl, p, np.minimum(th, 4080))
def setup_inputs_odd(rng):
    x, z, f, s, pl, p, th = parts(rng); h = W // 2
    o = np.argsort(rng.random((N, 8, W)), axis=-1)
    hi = np.zeros((N, 8, W), np.int64); np.put_along_axis(hi, o[:, :, h:], 1, 2)
    x = rng.integers(0, 56, (N, 8, 16, W)) + 200 * hi[:, :, None, :]; x[:, :, 15] ^= np.sum(x, axis=2) & 1
    kz = rng.integers(0, 2, (N, 8, 1, I)); z = rng.integers(0, 56, (N, 8, 16, I)) + 200 * kz; z[:, :, 15] ^= (np.sum(z, axis=2) & 1) ^ 1
    s = np.take_along_axis(o, (rng.integers(0, h, (N, 8, 16, I)) + h * (1 - kz)).reshape(N, 8, 16 * I), 2).reshape(N, 8, 16, I)
    pl = np.take_along_axis(o, (rng.integers(0, h, (N, 8, 16, PL)) + h * (np.arange(PL) & 1)).reshape(N, 8, 16 * PL), 2).reshape(N, 8, 16, PL)
    p = 2 * rng.integers(0, PL // 2, (N, 8, I)) + 1 - kz[:, :, 0]
    x[:, :, :, W - 1] = 255; x[:, ::2, :, W - 3] = 0; x[:, 1::2, :, 1] = 0
    pl[:, :, 0, PL - 1] = W - 1; pl[:, ::2, 0, 0] = W - 3; pl[:, 1::2, 0, 0] = 1
    ds = dist(records(x, s), z); dp = dist(records(x, np.take_along_axis(pl, p[:, :, None, :], 3)), z)
    one = (rng.random((N, 8, 16, I)) < 0.08).astype(np.int64); k = rng.integers(0, 3, (N, 8, 1, I))
    th = np.where(k == 0, ds + one, np.where(k == 1, np.minimum(dp + one, ds), np.minimum(dp, ds)))
    th = np.minimum(th, 4080)
    for i in (0, 1, I - 2, I - 1):
        z[:, :, :, i] = 0; f[:, :, :, i] = 0; s[:, :, 0, i] = W - 1; p[:, :, i] = PL - 1; th[:, :, :, i] = 0; th[:, :, 0, i] = 4080
    return pack(x, z, f, s, pl, p, th)
def setup_inputs_corners(rng):
    x, z, f, s, pl, p, th = parts(rng)
    k = rng.integers(0, 8, (N, 8, I)); k[:, :, I - 8:] = np.arange(8); k = k[:, :, None, :]; row = np.arange(16)[:, None]
    th = 4080 * ((((k == 1) | (k == 4) | (k == 5)) & (row == 15)) | ((k == 2) & (row == 0)) | (k == 3)).astype(np.int64)
    th = np.where(k == 7, rng.integers(0, 4081, (N, 8, 16, I)), th)
    z = np.where(k == 4, 255, np.where((k == 5) | (k == 7) | ((k == 0) & (rng.random((N, 8, 1, I)) < 0.5)), 0, z))
    z = np.where(k == 6, np.where(row == 1, 100, 15), z)
    s = np.where(k == 2, (W - 1) * rng.integers(0, 2, s.shape), s); s = np.where(k == 3, rng.integers(0, W, (N, 8, 1, I)), s)
    s = np.where(k == 7, 16 * np.arange(I) + rng.integers(0, 16, s.shape), s); s = np.where((k == 5) & (row == 15), W - 1, s)
    x[:, :, :, W - 1] = 255
    pl[:, :, :, 0] = rng.integers(0, W - 1, (N, 8, 1)); pl[:, :, :, PL - 1] = W - 1; pl[:, :, 15, :] = rng.integers(0, W - 1, (N, 8, PL))
    e = rng.integers(0, 4, (N, 8, I)); p = np.where(e == 0, 0, np.where(e == 1, PL - 1, p))
    return pack(x, z, f, s, pl, p, th)
def check_inputs(d):
    bad = []
    for k, lo, hi in (("x0", 0, 255), ("z0", 0, 255), ("f0", 0, 255), ("s0", 0, W - 1), ("pl", 0, W - 1), ("p0", 0, PL - 1), ("th", 0, 4080)):
        v = np.asarray(d[k]).astype(np.float64)
        if not np.all((v >= lo) & (v <= hi) & (v == np.floor(v))): bad.append("range of " + k)
    return bad
def reference(x0, z0, f0, s0, pl, p0, th):
    X = x0.astype(np.float32).astype(np.int32).reshape(N, 8, 16, W); z = z0.astype(np.float32).astype(np.int32).reshape(N, 8, 16, I); f = f0.astype(np.float32).astype(np.int32).reshape(N, 8, 16, I)
    S = s0.astype(np.int32).reshape(N, 8, 16, I); plans = pl.astype(np.int32).reshape(N, 8, 16, PL); lim = th.astype(np.int32).reshape(N, 8, 16, I)
    P = np.stack([gentries(a) for a in p0]).astype(np.int32); A = np.zeros((N, 8, I), np.int32)
    row = np.arange(16)[:, None]; wt = (2 * np.arange(16) + 1)[:, None]
    for t in range(RO):
        e = np.take_along_axis(plans, P[:, :, None, :], 3)
        xs = records(X, S); xe = records(X, e); bound = lim + AS * A[:, :, None, :]
        rs = dist(xs, z) < bound; rp = dist(xe, z) < bound
        c1 = np.any(rs, axis=2); c2 = ~c1 & np.any(rp, axis=2); c3 = ~c1 & ~c2
        j = np.argmax(rs, axis=2); jp = np.argmax(rp, axis=2)
        u = np.sum(wt * z, axis=2) & 4095; A = A + c3; P = np.where(c3, ((u * u >> 5) + 37 * u) & (PL - 1), P).astype(np.int32)
        low = np.sum(xs <= z[..., None], axis=2).transpose(0, 1, 3, 2)
        R = np.where(c1[:, :, None, :] & (low >= CNT) & (row != j[:, :, None, :]), e, S)
        t1 = np.take_along_axis(S, j[:, :, None, :], 2)[:, :, 0]; t2 = np.take_along_axis(e, jp[:, :, None, :], 2)[:, :, 0]; t3 = np.take_along_axis(plans[:, :, 0], P, 2)
        top = np.where(c1, t1, np.where(c2, t2, t3)); last = np.where(c1, j, 15)
        S = np.where(row <= last[:, :, None, :], np.concatenate([top[:, :, None, :], R[:, :, :15]], axis=2), R).astype(np.int32)
        f = (f + z) >> 1
        y = np.abs(np.take_along_axis(X, S[:, :, :1, :], 3) - f)
        place = 16 * np.arange(I) + (np.sum(y, axis=2) & 15)
        np.put_along_axis(X, place[:, :, None, :], (y + z) >> 1, 3)
        if t < RO - 1:
            z = np.concatenate([np.roll(y[..., b * B:(b + 1) * B], b + t, axis=0) for b in range(N)], axis=3)
    yx = np.sum(X.reshape(N, 8, 16, I, 16) * np.arange(1, 17), axis=4)
    return {"ys": S.reshape(N, 128, I).astype(np.float32), "yp": np.stack([gtable(a) for a in P + PL * A]).astype(np.float32),
            "yf": f.reshape(N, 128, I).astype(np.float32).astype(BF), "yx": yx.reshape(N, 128, I).astype(np.float32)}

@@ -1,0 +1,522 @@
+from concourse.bass import DstId, RemoteDMATransfer
+from concourse.mybir import AluOpType as A, ActivationFunctionType as F
+
+N, I, W, PLN, RO, B = 4, 192, 3072, 1024, 6, 48
+CH = [(0, 96), (96, 192)]
+NC = len(CH)
+PS = [False, True]
+LV = [True, True]
+PEC = 0.0005
+ZV = 8
+OFS = 1536
+
+SCRATCH = {
+    "pli": ("sbuf", [128, PLN], "int32"), "s0i": ("sbuf", [128, I], "int32"), "thi": ("sbuf", [128, I], "int32"),
+    "p0i": ("sbuf", [128, 12], "int32"), "f0b": ("sbuf", [128, I], "bfloat16"),
+    "X0": ("sbuf", [128, W], "bfloat16"), "X1": ("sbuf", [128, W], "bfloat16"),
+    "pid": ("sbuf", [128, 1], "int32"), "pmi": ("sbuf", [128, 1], "int32"), "cols": ("sbuf", [128, 16], "float32"),
+    "iC": ("sbuf", [128, I], "float32"), "iG": ("sbuf", [128, I], "float32"), "iM": ("sbuf", [128, I], "float32"),
+    "iB": ("sbuf", [128, 12], "float32"), "base": ("sbuf", [128, 12], "int32"),
+    "BD": ("sbuf", [128, 128], "bfloat16"), "BD64": ("sbuf", [128, 128], "bfloat16"), "IDb": ("sbuf", [128, 128], "bfloat16"),
+    "half": ("sbuf", [128, 128], "bfloat16"), "ones": ("sbuf", [128, I], "bfloat16"),
+    "LS": ("sbuf", [128, 128], "bfloat16"), "LI": ("sbuf", [128, 128], "bfloat16"), "tmpc": ("sbuf", [128, 128], "bfloat16"),
+    "tmpd": ("sbuf", [128, 128], "bfloat16"), "nIDb": ("sbuf", [128, 128], "bfloat16"), "WD2": ("sbuf", [128, 144], "bfloat16"),
+    "h_0": ("sbuf", [128, 96], "int32"), "Ho_0": ("sbuf", [128, 12], "uint16"), "tmpe": ("sbuf", [128, 128], "bfloat16"),
+    "WD": ("sbuf", [128, 144], "bfloat16"), "WD64": ("sbuf", [128, 144], "bfloat16"), "WD16": ("sbuf", [128, 144], "bfloat16"), "WU": ("sbuf", [128, 144], "bfloat16"),
+    "BDh": ("sbuf", [128, 128], "float16"), "R0h": ("sbuf", [128, 128], "float16"), "E00h": ("sbuf", [128, 128], "float16"),
+    "E0h": ("sbuf", [128, 128], "float16"), "IDh": ("sbuf", [128, 128], "float16"), "nIDh": ("sbuf", [128, 128], "float16"),
+    "ShI": ("sbuf", [128, 128], "float16"), "mk": ("sbuf", [128, I], "float32"), "rsh": ("sbuf", [128, I], "float16"),
+    "rsf": ("sbuf", [128, I], "float32"), "WI": ("sbuf", [128, 16 * 128], "bfloat16"),
+    "C3": ("sbuf", [128, RO * I], "bfloat16"), "phl": ("sbuf", [128, RO * 12], "int32"),
+    "Pl": ("sbuf", [128, 12], "float32"), "Pt": ("sbuf", [128, 12], "float32"), "Pt2": ("sbuf", [128, 12], "float32"),
+    "Al": ("sbuf", [128, 12], "float32"), "ypo": ("sbuf", [128, 12], "float32"), "P0u": ("sbuf", [128, 12], "uint16"),
+    "yso": ("sbuf", [128, I], "float32"), "yfo": ("sbuf", [128, I], "bfloat16"), "yxo": ("sbuf", [128, I], "float32"),
+}
+for _t in range(RO):
+    SCRATCH["Z%d" % _t] = ("sbuf", [128, I], "bfloat16")
+    SCRATCH["Y%d" % _t] = ("sbuf", [128, I], "bfloat16")
+for _c, (_a, _b) in enumerate(CH):
+    _n = _b - _a
+    for _nm, _sh, _dt in (("ZR", [16 * _n], "bfloat16"), ("dS", [16 * _n], "bfloat16"), ("dP", [16 * _n], "bfloat16"), ("aS", [16 * _n], "bfloat16"),
+                          ("aP", [16 * _n], "bfloat16"), ("lo", [16 * _n], "bfloat16"), ("E0", [3 * _n], "float16"), ("E1", [3 * _n], "float16"),
+                          ("So", [_n], "uint16"), ("Eo", [_n], "uint16"), ("fb", [_n], "float16"), ("bd", [_n], "float32"),
+                          ("rl", [2 * _n], "bfloat16"), ("hm", [2 * _n], "bfloat16"), ("Wm", [3 * _n], "float16"), ("lb", [_n], "float16"),
+                          ("R", [_n], "float16"), ("tm", [_n], "float16"), ("ts", [_n], "float16"), ("y0", [_n], "float32"), ("v", [_n], "int32"),
+                          ("pm", [_n], "float32"), ("ps", [_n], "int32"), ("pl", [48], "int32"),
+                          ("To", [12], "uint16"), ("Po", [12], "uint16")):
+        SCRATCH["%s_%d" % (_nm, _c)] = ("sbuf", [128] + _sh, _dt)
+for _k in range(8):
+    SCRATCH["B%d" % _k] = ("psum", [128, 512], "float32")
+
+LOADS = ["x0", "s0", "z0", "pl", "p0", "f0", "th"]
+SEMAPHORES = ["V", "S", "P", "G", "sent"] + ["ld_" + k for k in LOADS] + ["xc%d" % t for t in range(RO)] + ["o%d" % k for k in range(8)]
+SEMAPHORES += ["a%d_%d" % (t, b) for t in range(RO - 1) for b in range(4) if (b + t) % 4]
+
+CY = 0.00083
+
+
+class _Nothing:
+    pass
+
+
+def schedule(ops, eng_list):
+    n = len(ops)
+    succ = [[] for _ in range(n)]
+    for i, o in enumerate(ops):
+        for d in o["dep"]:
+            succ[d].append(i)
+    lat = 0.08
+    prio = [0.0] * n
+    for i in range(n - 1, -1, -1):
+        m = 0.0
+        for s in succ[i]:
+            x = prio[s] + (lat if ops[s]["e"] != ops[i]["e"] else 0.03)
+            if x > m:
+                m = x
+        prio[i] = m + ops[i]["c"] + ops[i]["x"]
+    left = [len(o["dep"]) for o in ops]
+    ready = {}
+    for e in eng_list:
+        ready[e] = []
+    when = [0.0] * n
+    est = [0.0] * n
+    for i, o in enumerate(ops):
+        if not left[i]:
+            ready[o["e"]].append(i)
+    free = {}
+    for e in eng_list:
+        free[e] = 0.0
+    order = []
+    while len(order) < n:
+        best = None
+        for e in eng_list:
+            if not ready[e]:
+                continue
+            f = free[e]
+            lowest = min(max(f, est[i]) for i in ready[e])
+            cand = [i for i in ready[e] if max(f, est[i]) <= lowest + 0.02]
+            j = max(cand, key=lambda i: prio[i])
+            k = (max(f, est[j]), -prio[j], j)
+            if best is None or k < best:
+                best = k
+        st, _, j = best
+        o = ops[j]
+        ready[o["e"]].remove(j)
+        order.append(j)
+        if o["e"] != "N":
+            free[o["e"]] = st + o["c"]
+        when[j] = st + o["c"] + o["x"]
+        for s in succ[j]:
+            left[s] -= 1
+            x = when[j] + (lat if ops[s]["e"] != o["e"] else 0.03)
+            if x > est[s]:
+                est[s] = x
+            if not left[s]:
+                ready[ops[s]["e"]].append(s)
+    return order, when
+
+
+def rank_program(g, core, T, topo):
+    rank = T.rank_of(core)
+    if rank is None:
+        return
+    ops = []
+    last_w, last_r = {}, {}
+    banks = {}
+    queue = {"V": g.vector, "S": g.scalar, "P": g.tensor, "G": g, "Y": g.sync, "N": None}
+
+    def op(e, c, fn, r=(), w=(), sem=None, x=0.0, inc=None):
+        i = len(ops)
+        dep = {}
+
+        def need(j, raw):
+            if j != i:
+                dep[j] = dep.get(j, False) or raw
+        for k in r:
+            if k in last_w:
+                need(last_w[k], True)
+        for k in w:
+            if k in last_w:
+                need(last_w[k], False)
+            for j in last_r.get(k, ()):
+                need(j, False)
+        bs = set(k[:2] for k in tuple(r) + tuple(w) if k[0] == "B" and k[2:3] == ".")
+        for b in bs:
+            cur = banks.setdefault(b, [e, [], []])
+            if cur[0] != e:
+                cur[0], cur[1], cur[2] = e, cur[2], []
+            for j in cur[1]:
+                need(j, False)
+            cur[2].append(i)
+        for k in r:
+            last_r.setdefault(k, []).append(i)
+        for k in w:
+            last_w[k] = i
+            last_r[k] = []
+        ops.append({"e": e, "c": c, "x": x, "fn": fn, "dep": dep, "sem": sem, "inc": inc})
+        return i
+
+    def V(n, fn, r, w, f=1.0):
+        op("V", max(64, n * f) * CY, lambda: fn(g.vector), r, w)
+
+    def VG(n, fn, r, w):
+        op("V", 0.05 + n * 1.5 * CY, lambda: fn(g.vector), r, w)
+
+    def S(n, fn, r, w):
+        op("S", 0.06 + n * CY, lambda: fn(g.scalar), r, w)
+
+    def P(mms, r, w, first=True, last=True):
+        def fn():
+            k = len(mms)
+            for j, (o, l, rr, n) in enumerate(mms):
+                ins = g.tensor.matmul(o, l, rr, first and j == 0, last and j == k - 1)
+            return ins
+        op("P", sum(max(64, m[3]) for m in mms) * PEC, fn, r, w)
+
+    def load(e, name, dst, w, x):
+        op(e, 0.1, lambda: queue[e].dma_start(dst, T[name][:]), (), w, sem="ld_" + name, x=x)
+    ZK = lambda t: ["Z%d.%d" % (t, b) for b in range(4)]
+    load("Y", "x0", T.X0[:], ["X.0.%d" % c for c in range(NC)], 4.5)
+    load("S", "p0", T.p0i[:], ["p0i"], 2.0)
+    load("S", "pl", T.pli[:], ["pli"], 3.0)
+    load("Y", "s0", T.s0i[:], ["s0i"], 2.5)
+    load("S", "z0", T.Z0[:], ZK(0), 2.2)
+    load("Y", "th", T.thi[:], ["thi"], 2.5)
+    load("S", "f0", T.f0b[:], ["f0b"], 2.2)
+
+    op("G", 0.15, lambda: g.iota(T.pid[:], [[1, 1]], 0, 1), (), ["pid"])
+    op("G", 0.5, lambda: g.iota(T.iC[:], [[1, I]], 0, 0, allow_small_or_imprecise_dtypes=True), (), ["iC"])
+    op("G", 0.5, lambda: g.iota(T.iG[:], [[16, 12], [0, 16]], 0, 0, allow_small_or_imprecise_dtypes=True), (), ["iG"])
+    op("G", 0.5, lambda: g.iota(T.iM[:], [[0, 12], [1, 16]], 0, 0, allow_small_or_imprecise_dtypes=True), (), ["iM"])
+    op("G", 0.2, lambda: g.iota(T.iB[:], [[256, 12]], 0, 0, allow_small_or_imprecise_dtypes=True), (), ["iB"])
+    col = lambda k: T.cols[:, k:k + 1]
+    V(128, lambda v: v.memset(T.half[:], 0.5), (), ["half"])
+    V(192, lambda v: v.memset(T.ones[:], 1.0), (), ["ones"])
+    V(1, lambda v: v.tensor_scalar(T.pmi[:], T.pid[:], 15, None, A.bitwise_and), ["pid"], ["pmi"])
+    V(1, lambda v: v.tensor_copy(col(0), T.pid[:]), ["pid"], ["c0"])
+    V(1, lambda v: v.tensor_copy(col(1), T.pmi[:]), ["pmi"], ["c1"])
+    V(1, lambda v: v.tensor_tensor(col(2), col(0), col(1), A.subtract), ["c0", "c1"], ["c2"])
+    V(1, lambda v: v.tensor_scalar(col(3), col(2), 15.0, None, A.add), ["c2"], ["c3"])
+    V(1, lambda v: v.tensor_scalar(col(4), col(0), 1.0, None, A.add), ["c0"], ["c4"])
+    V(1, lambda v: v.tensor_scalar(col(5), col(1), 0.0, None, A.is_equal), ["c1"], ["c5"])
+    V(1, lambda v: v.tensor_scalar(col(6), col(1), 2.0, 1.0, A.mult, A.add), ["c1"], ["c6"])
+    V(1, lambda v: v.tensor_scalar(col(7), col(1), 16.0, None, A.mult), ["c1"], ["c7"])
+
+    def cs(out, src, n, c, o0, r, w):
+        V(n, lambda v: v.tensor_scalar(out, src, c, None, o0), r, w)
+    cs(T.WD[:], T.iC[:, 0:144], 144, col(3), A.is_equal, ["iC", "c3"], ["WD"])
+    cs(T.WU[:], T.WD[:], 144, col(6), A.mult, ["WD", "c6"], ["WU"])
+    cs(T.WD64[:], T.WD[:], 72, 1.0 / 64, A.mult, ["WD"], ["WD64"])
+    cs(T.WD16[:], T.WD[:], 72, 1.0 / 16, A.mult, ["WD"], ["WD16"])
+    cs(T.BD[:], T.iG[:, 0:128], 128, col(2), A.is_equal, ["iG", "c2"], ["BD"])
+    cs(T.IDb[:], T.iC[:, 0:128], 128, col(0), A.is_equal, ["iC", "c0"], ["IDb"])
+    cs(T.mk[:], T.iM[:], 192, col(1), A.is_equal, ["iM", "c1"], ["mk"])
+    cs(T.rsh[:], T.iM[:], 192, 0.0, A.is_gt, ["iM"], ["rsh"])
+    cs(T.rsf[:], T.iM[:], 192, 0.0, A.is_gt, ["iM"], ["rsf"])
+    cs(T.tmpc[:], T.iC[:, 0:128], 128, col(0), A.is_gt, ["iC", "c0"], ["tmpc"])
+    V(256, lambda v: v.tensor_tensor(T.LS[:], T.tmpc[:], T.BD[:], A.mult), ["tmpc", "BD"], ["LS"])
+    cs(T.tmpd[:], T.IDb[:], 64, 64.0, A.mult, ["IDb"], ["tmpd"])
+    V(256, lambda v: v.tensor_tensor(T.LI[:], T.LS[:], T.tmpd[:], A.subtract), ["LS", "tmpd"], ["LI"])
+    cs(T.IDh[:], T.IDb[:], 64, 1.0, A.mult, ["IDb"], ["IDh"])
+    cs(T.nIDb[:], T.IDb[:], 64, -1.0, A.mult, ["IDb"], ["nIDb"])
+    cs(T.WD2[:], T.WD[:], 72, 2.0, A.mult, ["WD"], ["WD2"])
+    cs(T.nIDh[:], T.IDb[:], 64, -1.0, A.mult, ["IDb"], ["nIDh"])
+    cs(T.BD64[:], T.BD[:], 64, 64.0, A.mult, ["BD"], ["BD64"])
+    cs(T.BDh[:], T.BD[:], 64, 1.0, A.mult, ["BD"], ["BDh"])
+    cs(T.R0h[:], T.BD[:], 64, col(5), A.mult, ["BD", "c5"], ["R0h"])
+    cs(T.E00h[:], T.IDb[:], 64, col(5), A.mult, ["IDb", "c5"], ["E00h"])
+    cs(T.E0h[:], T.WD[:, 15:143], 64, 1.0, A.mult, ["WD"], ["E0h"])
+    cs(T.tmpe[:], T.iC[:, 0:128], 128, col(4), A.is_equal, ["iC", "c4"], ["tmpe"])
+    V(256, lambda v: v.tensor_tensor(T.tmpe[:], T.tmpe[:], T.BD[:], A.mult), ["tmpe", "BD"], ["tmpe"])
+    V(256, lambda v: v.tensor_tensor(T.ShI[:], T.tmpe[:], T.IDb[:], A.subtract), ["tmpe", "IDb"], ["ShI"])
+    cs(T.base[:], T.iB[:], 12, col(7), A.add, ["iB", "c7"], ["base"])
+
+    V(12, lambda v: v.tensor_copy(T.P0u[:], T.p0i[:]), ["p0i"], ["P0u"])
+    V(12, lambda v: v.tensor_copy(T.Pl[:], T.p0i[:]), ["p0i"], ["Pl"])
+    for c, (lo, hi) in enumerate(CH):
+        n = hi - lo
+        b = lambda nm, c=c: T["%s_%d" % (nm, c)]
+        K = lambda nm, c=c: "%s_%d" % (nm, c)
+        V(n, lambda v, b=b, lo=lo, hi=hi: v.tensor_copy(b("So")[:], T.s0i[:, lo:hi]), ["s0i"], [K("So")])
+        V(n, lambda v, b=b, lo=lo, hi=hi, n=n: v.tensor_scalar(b("E0")[:, 2 * n:3 * n], T.s0i[:, lo:hi], -float(OFS), None, A.add), ["s0i"], [K("S0")])
+        if lo % 32 == 0:
+            pu, pk = (lambda lo=lo, hi=hi: T.P0u[:, lo // 16:hi // 16]), "P0u"
+        else:
+            V(n, lambda v, b=b, lo=lo, hi=hi: v.tensor_copy(b("Po")[:, 0:(hi - lo) // 16], T.p0i[:, lo // 16:hi // 16]), ["p0i"], [K("Po")])
+            pu, pk = (lambda b=b, n=n: b("Po")[:, 0:n // 16]), K("Po")
+        VG(n, lambda v, b=b, n=n, pu=pu: v.tensor_scalar(b("E0")[:, n:2 * n], T.pli[:, :].indirect(pu()), -float(OFS), None, A.add), ["pli", pk], [K("e0")])
+        V(n, lambda v, b=b, n=n: v.tensor_scalar(b("Eo")[:], b("E0")[:, n:2 * n], float(OFS), None, A.add), [K("e0")], [K("Eo")], 0.5)
+        V(n, lambda v, b=b, lo=lo, hi=hi: v.tensor_scalar(b("fb")[:], T.f0b[:, lo:hi], 1024.0, None, A.add), ["f0b"], [K("fb")], 0.5)
+        V(n, lambda v, b=b, lo=lo, hi=hi: v.tensor_scalar(b("bd")[:], T.thi[:, lo:hi], 1.0 / 64, None, A.mult), ["thi"], [K("bd")])
+
+    win = lambda nm, k: T[nm][:, 15 - k:143 - k]
+
+    def zprep(t, c):
+        lo, hi = CH[c]
+        n, m = hi - lo, (hi - lo) // 16
+        b = lambda nm: T["%s_%d" % (nm, c)]
+        K = lambda nm: "%s_%d" % (nm, c)
+        Z = T["Z%d" % t]
+        zk = ["Z%d.%d" % (t, k) for k in range(lo // B, hi // B)]
+        for k in range(16):
+            if k < ZV:
+                V(n, lambda v, k=k: v.tensor_copy(b("ZR")[:, k:16 * n:16], Z[:, lo:hi]), zk, [K("ZR") + ".%d" % k], 0.5)
+            else:
+                S(n, lambda s, k=k: s.activation(b("ZR")[:, k:16 * n:16], Z[:, lo:hi], F.Copy), zk, [K("ZR") + ".%d" % k])
+        P([(T.B7[:, 0:n], T.IDh[:], b("fb")[:], n), (T.B7[:, 0:n], T.IDb[:], Z[:, lo:hi], n)], [K("fb"), "IDh", "IDb"] + zk, ["B7.f"])
+        V(n, lambda v: v.tensor_scalar(b("fb")[:], T.B7[:, 0:n], 0.5, 511.75, A.mult, A.add), ["B7.f"], [K("fb")])
+
+    def zhash(t):
+        m = 12
+        Z = T["Z%d" % t]
+        P([(T.B7[:, 256:256 + m], win("WU", k), Z[:, k:I:16], m) for k in range(16)], ["WU"] + ZK(t), ["B7.u"])
+        h = lambda k: T.h_0[:, 12 * k:12 * k + m]
+        H = lambda k: "h.%d" % k
+        ph = T.phl[:, 12 * t:12 * t + 12]
+        V(m, lambda v: v.tensor_copy(h(0), T.B7[:, 256:256 + m]), ["B7.u"], [H(0)])
+        V(m, lambda v: v.tensor_scalar(h(1), h(0), 4095, None, A.bitwise_and), [H(0)], [H(1)])
+        V(m, lambda v: v.tensor_tensor(h(2), h(1), h(1), A.mult), [H(1)], [H(2)])
+        V(m, lambda v: v.tensor_scalar(h(4), h(1), 37.0, None, A.mult), [H(1)], [H(4)])
+        V(m, lambda v: v.tensor_scalar(h(3), h(2), 5, None, A.logical_shift_right), [H(2)], [H(3)])
+        V(m, lambda v: v.tensor_tensor(h(5), h(3), h(4), A.add), [H(3), H(4)], [H(5)])
+        V(m, lambda v: v.tensor_scalar(ph, h(5), 1023, None, A.bitwise_and), [H(5)], ["ph%d" % t])
+        V(m, lambda v: v.tensor_copy(T.Ho_0[:], ph), ["ph%d" % t], ["Ho"])
+        for c, (lo, hi) in enumerate(CH):
+            VG(hi - lo, lambda v, c=c, lo=lo, hi=hi: v.tensor_scalar(T["E%d_%d" % (t % 2, c)][:, 0:hi - lo], T.pli[:, :].indirect(T.Ho_0[:, lo // 16:hi // 16]), -float(OFS), None, A.add),
+               ["pli", "Ho"], ["eh%d_%d" % (t % 2, c)])
+
+    def bulk(t, c):
+        lo, hi = CH[c]
+        n = hi - lo
+        b = lambda nm: T["%s_%d" % (nm, c)]
+        K = lambda nm: "%s_%d" % (nm, c)
+        X = T["X%d" % (t % 2)]
+        xk = ["X.%d.%d" % (t % 2, k) for k in range(NC)]
+        ks = range(lo // B, hi // B)
+        for dst, of in (("dS", "So"), ("dP", "Eo")):
+            for k in ks:
+                u = k * B - lo
+                if dst == "dP" and PS[c]:
+                    op("S", 0.065 + 16 * B * 1.5 * CY, lambda dst=dst, of=of, u=u: g.scalar.activation(b(dst)[:, 16 * u:16 * (u + B)], X[:, :].indirect(b(of)[:, u:u + B]), F.Copy),
+                       xk + [K(of)], [K(dst) + ".%d" % k])
+                    continue
+                VG(16 * B, lambda v, dst=dst, of=of, u=u: v.tensor_tensor(b(dst)[:, 16 * u:16 * (u + B)], X[:, :].indirect(b(of)[:, u:u + B]), b("ZR")[:, 16 * u:16 * (u + B)], A.subtract),
+                   xk + [K(of)] + [K("ZR") + ".%d" % j for j in range(16)], [K(dst) + ".%d" % k])
+        for k in ks:
+            sl = slice(16 * (k * B - lo), 16 * (k * B - lo + B))
+            S(16 * B, lambda s, sl=sl: s.activation(b("aS")[:, sl], b("dS")[:, sl], F.Abs), [K("dS") + ".%d" % k], [K("aS") + ".%d" % k])
+            if not PS[c]:
+                S(16 * B, lambda s, sl=sl: s.activation(b("aP")[:, sl], b("dP")[:, sl], F.Abs), [K("dP") + ".%d" % k], [K("aP") + ".%d" % k])
+            if LV[c]:
+                V(16 * B, lambda v, sl=sl: v.tensor_scalar(b("lo")[:, sl], b("dS")[:, sl], 0.0, None, A.is_le), [K("dS") + ".%d" % k], [K("lo") + ".%d" % k], 0.5)
+            else:
+                S(16 * B, lambda s, sl=sl: s.activation(b("lo")[:, sl], b("dS")[:, sl], F.Sign, bias=0.5, scale=-1.0), [K("dS") + ".%d" % k], [K("lo") + ".%d" % k])
+        if PS[c]:
+            Z = T["Z%d" % t]
+            zk = ["Z%d.%d" % (t, k) for k in ks]
+            for j in range(4):
+                bn = "B%d" % (1 + j % 2)
+                d = T[bn]
+
+                def sub(j=j, d=d):
+                    for q in range(4):
+                        g.tensor.matmul(d[:, q * n:q * n + n], T.IDb[:], b("dP")[:, 4 * j + q:16 * n:16], True, False)
+                        ins = g.tensor.matmul(d[:, q * n:q * n + n], T.nIDb[:], Z[:, lo:hi], False, True)
+                    return ins
+                op("P", 8 * n * PEC, sub, ["IDb", "nIDb"] + zk + [K("dP") + ".%d" % k for k in ks], [bn + ".d"])
+                S(4 * n, lambda s, j=j, d=d: s.activation(b("aP")[:, 4 * j * n:4 * (j + 1) * n], d[:, 0:4 * n], F.Abs), [bn + ".d"], [K("aP") + ".j%d" % j])
+
+    def reduce(t, c):
+        lo, hi = CH[c]
+        n = hi - lo
+        b = lambda nm: T["%s_%d" % (nm, c)]
+        K = lambda nm: "%s_%d" % (nm, c)
+        q = lambda nm: [K(nm) + ".%d" % k for k in range(lo // B, hi // B)]
+        P([(T.B0[:, n:2 * n], win("WD64", k), b("aS")[:, k:16 * n:16], n) for k in range(16)], ["WD64"] + q("aS"), ["B0.S"])
+        if PS[c]:
+            for j in range(4):
+                P([(T.B0[:, 0:n], win("WD64", k), b("aP")[:, k * n:k * n + n], n) for k in range(4 * j, 4 * j + 4)], ["WD64", K("aP") + ".j%d" % j, "B0.P" if j else "B0.S"], ["B0.P"],
+                  first=j == 0, last=j == 3)
+        else:
+            P([(T.B0[:, 0:n], win("WD64", k), b("aP")[:, k:16 * n:16], n) for k in range(16)], ["WD64"] + q("aP"), ["B0.P"])
+
+    def control(t, c):
+        lo, hi = CH[c]
+        n, m = hi - lo, (hi - lo) // 16
+        b = lambda nm: T["%s_%d" % (nm, c)]
+        K = lambda nm: "%s_%d" % (nm, c)
+        par, nxt = t % 2, (t + 1) % 2
+        E, En = b("E%d" % par), b("E%d" % nxt)
+        kS, ke, keh = K("S%d" % par), K("e%d" % par), K("eh%d" % par)
+        X, Xn = T["X%d" % par], T["X%d" % nxt]
+        xk = ["X.%d.%d" % (par, k) for k in range(NC)]
+        Z, Y = T["Z%d" % t], T["Y%d" % t]
+        zk = ["Z%d.%d" % (t, k) for k in range(lo // B, hi // B)]
+        bk = "B0"
+        D = T[bk]
+        last = t == RO - 1
+        P([(T.B6[:, 0:n], T.IDh[:], E[:, n:2 * n], n), (T.B6[:, 0:n], T.nIDh[:], E[:, 2 * n:3 * n], n)], [kS, ke, "IDh", "nIDh"], ["B6.d"])
+        if not last:
+            P([(T.B6[:, n:2 * n], T.IDh[:], E[:, 0:n], n), (T.B6[:, n:2 * n], T.nIDh[:], E[:, n:2 * n], n)], [keh, ke, "IDh", "nIDh"], ["B6.e"])
+        rl = b("rl")
+        V(n, lambda v: v.tensor_tensor(rl[:, n:2 * n], D[:, n:2 * n], b("bd")[:], A.is_lt), [bk + ".S", K("bd")], [K("rS")])
+        V(n, lambda v: v.tensor_tensor(rl[:, 0:n], D[:, 0:n], b("bd")[:], A.is_lt), [bk + ".P", K("bd")], [K("rP")])
+        B3 = T.B3
+        rr = [K("rS"), K("rP")]
+        P([(B3[:, n:3 * n], T.half[:], T.ones[:, 0:2 * n], 2 * n), (B3[:, n:3 * n], T.LI[:], rl[:, 0:2 * n], 2 * n), (B3[:, n:2 * n], T.BD[:], rl[:, n:2 * n], n)],
+          rr + ["half", "ones", "LI", "BD"], ["B3.h"])
+        P([(B3[:, 0:n], T.BD[:], rl[:, n:2 * n], n), (B3[:, 0:n], T.BD[:], rl[:, 0:n], n)], rr + ["BD"], ["B3.t"])
+        P([(B3[:, 3 * n:4 * n], T.LS[:], rl[:, n:2 * n], n)], [K("rS"), "LS"], ["B3.m"])
+        S(3 * n, lambda s: s.activation(T.B4[:, 0:3 * n], B3[:, 0:3 * n], F.Relu, bias=1.0, scale=-1.0), ["B3.h", "B3.t"], ["B4.h"])
+        S(2 * n, lambda s: s.activation(b("hm")[:], B3[:, 2 * n:4 * n], F.Relu, bias=1.0, scale=-1.0), ["B3.h", "B3.m"], [K("hm")])
+        c3 = T.C3[:, t * I + lo:t * I + hi]
+        S(n, lambda s: s.activation(c3, B3[:, 0:n], F.Relu, bias=1.0, scale=-1.0), ["B3.t"], ["C3_%d_%d" % (t, c)])
+        Wm = b("Wm")
+        V(3 * n, lambda v: v.tensor_tensor(Wm[:], E[:], T.B4[:, 0:3 * n], A.mult), [kS, ke, keh, "B4.h"], [K("Wm")])
+        P([(T.B5[:, 0:n], T.R0h[:], Wm[:, 0:n], n), (T.B5[:, 0:n], T.BDh[:], Wm[:, n:2 * n], n), (T.B5[:, 0:n], T.BDh[:], Wm[:, 2 * n:3 * n], n)],
+          [K("Wm"), "R0h", "BDh"], ["B5.t"])
+        V(n, lambda v: v.tensor_tensor(b("tm")[:], T.B5[:, 0:n], T.mk[:, 0:n], A.mult), ["B5.t", "mk"], [K("tm")])
+        V(n, lambda v: v.tensor_tensor_scan(b("ts")[:], T.rsh[:, 0:n], b("tm")[:], 0.0, A.mult, A.add), [K("tm"), "rsh"], [K("ts")], 0.5)
+        V(m, lambda v: v.tensor_scalar(b("To")[:, 0:m], b("ts")[:, 15:n:16], float(OFS), None, A.add), [K("ts")], [K("To")])
+        VG(n, lambda v: v.tensor_tensor(b("y0")[:], X[:, :].indirect(b("To")[:, 0:m]), b("fb")[:], A.subtract), xk + [K("To"), K("fb")], [K("y0")])
+        yk = ["Y%d.%d" % (t, k) for k in range(lo // B, hi // B)]
+        S(n, lambda s: s.activation(Y[:, lo:hi], b("y0")[:], F.Abs, bias=1024.0), [K("y0")], yk)
+        if not last:
+            go = [k for k in range(lo // B, hi // B) if (k + t) % 4]
+            stay = [k for k in range(lo // B, hi // B) if (k + t) % 4 == 0]
+            for k in stay:
+                V(B, lambda v, k=k: v.tensor_copy(T["Z%d" % (t + 1)][:, k * B:k * B + B], Y[:, k * B:k * B + B]), ["Y%d.%d" % (t, k)], ["Z%d.%d" % (t + 1, k)])
+            cnt = 8 // len(go) if len(go) in (1, 2) else 2
+
+            def send():
+                tr = []
+                for q, k in enumerate(go):
+                    dst = T.cores[(rank + k + t) % N]
+                    rid, pc = topo.addr(dst, core)
+                    es = topo.engines(core, dst)[q * cnt:(q + 1) * cnt]
+                    tr.append(RemoteDMATransfer(dst_ids=[DstId(rid=rid, pnc=pc)], dma_engine_mask=sum(1 << x for x in es), remote_sem=T.sem["a%d_%d" % (t, k)],
+                                                src=Y[:, k * B:k * B + B], dst=T["Z%d" % (t + 1)][:, k * B:k * B + B]))
+                g.remote_dma_fused(tr, local_sem=T.sem.sent)
+            op("G", 1.0, send, ["Y%d.%d" % (t, k) for k in go], ["net"], sem="sent", inc=cnt * len(go))
+            for k in go:
+                op("N", 0.0, None, ["net"], ["Z%d.%d" % (t + 1, k)], sem="a%d_%d" % (t, k), inc=cnt, x=3.0)
+        P([(T.B5[:, n:2 * n], T.BD[:], Y[:, lo:hi], n)], yk + ["BD"], ["B5.y"])
+        V(n, lambda v: v.tensor_tensor(b("pm")[:], T.B5[:, n:2 * n], T.mk[:, 0:n], A.mult), ["B5.y", "mk"], [K("pm")])
+        V(n, lambda v: v.tensor_tensor_scan(b("ps")[:], T.rsf[:, 0:n], b("pm")[:], 0.0, A.mult, A.add), [K("pm"), "rsf"], [K("ps")])
+        p = lambda k: b("pl")[:, 12 * k:12 * k + m]
+        V(m, lambda v: v.tensor_scalar(p(0), b("ps")[:, 15:n:16], 15, None, A.bitwise_and), [K("ps")], [K("p0")])
+        V(m, lambda v: v.tensor_tensor(p(1), p(0), T.base[:, lo // 16:hi // 16], A.add), [K("p0"), "base"], [K("p1")])
+        V(m, lambda v: v.tensor_copy(b("Po")[:, 0:m], p(1)), [K("p1")], [K("Po")])
+        hm = b("hm")
+        lw = "WD2" if LV[c] else "WD"
+        P([(T.B0[:, 2 * n:3 * n], T.BD64[:], hm[:, 0:n], n)] + [(T.B0[:, 2 * n:3 * n], win(lw, k), b("lo")[:, k:16 * n:16], n) for k in range(16)],
+          [K("hm"), "BD64", lw] + [K("lo") + ".%d" % k for k in range(lo // B, hi // B)], ["B0.l"])
+        V(n, lambda v: v.tensor_scalar(b("lb")[:], T.B0[:, 2 * n:3 * n], 86.0 if LV[c] else 70.0, None, A.is_ge), ["B0.l"], [K("lb")])
+        V(n, lambda v: v.tensor_tensor(T.B6[:, 0:n], T.B6[:, 0:n], b("lb")[:], A.mult), ["B6.d", K("lb")], ["B6.d"])
+        V(n, lambda v: v.tensor_tensor(b("R")[:], E[:, 2 * n:3 * n], T.B6[:, 0:n], A.add), ["B6.d", kS], [K("R")])
+        if not last:
+            V(n, lambda v: v.tensor_tensor(T.B6[:, n:2 * n], T.B6[:, n:2 * n], c3, A.mult), ["B6.e", "C3_%d_%d" % (t, c)], ["B6.e"])
+            V(n, lambda v: v.tensor_tensor(En[:, n:2 * n], E[:, n:2 * n], T.B6[:, n:2 * n], A.add), ["B6.e", ke], [K("e%d" % nxt)])
+            V(n, lambda v: v.tensor_scalar(b("Eo")[:], En[:, n:2 * n], float(OFS), None, A.add), [K("e%d" % nxt)], [K("Eo")], 0.5)
+            V(n, lambda v: v.tensor_tensor(b("bd")[:], b("bd")[:], T.B4[:, 0:n], A.add), ["B4.h", K("bd")], [K("bd")])
+        P([(T.B6[:, 2 * n:3 * n], T.ShI[:], b("R")[:], n), (T.B6[:, 2 * n:3 * n], T.E00h[:], Wm[:, 0:n], n), (T.B6[:, 2 * n:3 * n], T.E0h[:], Wm[:, n:2 * n], n),
+           (T.B6[:, 2 * n:3 * n], T.E0h[:], Wm[:, 2 * n:3 * n], n)], [K("R"), K("Wm"), "ShI", "E00h", "E0h"], ["B6.s"])
+        P([(T.B6[:, 3 * n:4 * n], T.IDb[:], Y[:, lo:hi], n), (T.B6[:, 3 * n:4 * n], T.IDb[:], Z[:, lo:hi], n)], yk + zk + ["IDb"], ["B6.y"])
+        V(n, lambda v: v.tensor_scalar(b("v")[:], T.B6[:, 3 * n:4 * n], 0.5, -0.25, A.mult, A.add), ["B6.y"], [K("v")])
+        op("V", 0.05 + n * 3 * CY, lambda: g.vector.tensor_copy(Xn[:, :].indirect(b("Po")[:, 0:m]), b("v")[:]), [K("v"), K("Po"), "X.%d.all" % nxt], ["X.%d.%d" % (nxt, c)])
+        V(n, lambda v: v.tensor_tensor(T.B6[:, 2 * n:3 * n], T.B6[:, 2 * n:3 * n], hm[:, n:2 * n], A.mult), ["B6.s", K("hm")], ["B6.s"])
+        V(n, lambda v: v.tensor_tensor(En[:, 2 * n:3 * n], b("R")[:], T.B6[:, 2 * n:3 * n], A.add), ["B6.s", K("R")], [K("S%d" % nxt)])
+        if not last:
+            V(n, lambda v: v.tensor_scalar(b("So")[:], En[:, 2 * n:3 * n], float(OFS), None, A.add), [K("S%d" % nxt)], [K("So")], 0.5)
+        else:
+            V(n, lambda v: v.tensor_scalar(T.yso[:, lo:hi], En[:, 2 * n:3 * n], float(OFS), None, A.add), [K("S%d" % nxt)], ["yso%d" % c])
+
+    def copyX(t):
+        par, nxt = t % 2, (t + 1) % 2
+        op("Y", 0.1, lambda: g.sync.dma_start(T["X%d" % nxt][:], T["X%d" % par][:]), ["X.%d.%d" % (par, k) for k in range(NC)],
+           ["X.%d.%d" % (nxt, k) for k in range(NC)] + ["X.%d.all" % nxt], sem="xc%d" % t, x=4.5)
+
+    def plans(t0, t1):
+        w = 12 * (t1 - t0)
+        P([(T.B7[:, 0:w], win("WD16", k), T.C3[:, t0 * I + k:t1 * I:16], w) for k in range(16)], ["WD16"] + ["C3_%d_%d" % (t, c) for t in range(t0, t1) for c in range(NC)], ["B7.f"])
+        for t in range(t0, t1):
+            q = T.B7[:, 12 * (t - t0):12 * (t - t0 + 1)]
+            ph = T.phl[:, 12 * t:12 * t + 12]
+            V(12, lambda v, ph=ph: v.tensor_tensor(T.Pt[:], ph, T.Pl[:], A.subtract), ["Pl", "ph%d" % t], ["Pt"])
+            V(12, lambda v, q=q: v.tensor_tensor(T.Pt2[:], T.Pt[:], q, A.mult), ["Pt", "B7.f"], ["Pt2"])
+            V(12, lambda v: v.tensor_tensor(T.Pl[:], T.Pl[:], T.Pt2[:], A.add), ["Pt2", "Pl"], ["Pl"])
+            if t == 0:
+                V(12, lambda v, q=q: v.tensor_copy(T.Al[:], q), ["B7.f"], ["Al"])
+            else:
+                V(12, lambda v, q=q: v.tensor_tensor(T.Al[:], T.Al[:], q, A.add), ["B7.f", "Al"], ["Al"])
+
+    for c in range(NC):
+        zprep(0, c)
+    zhash(0)
+    for t in range(RO):
+        for c in range(NC):
+            bulk(t, c)
+        copyX(t)
+        if t == RO - 1:
+            plans(0, t)
+            for k in range(16):
+                cs(T.WI[:, 128 * k:128 * k + 128], T.IDb[:], 64, float(k + 1), A.mult, ["IDb"], ["WI%d" % k])
+            for c, (lo, hi) in enumerate(CH):
+                V(hi - lo, lambda v, c=c, lo=lo, hi=hi: v.tensor_scalar(T.yfo[:, lo:hi], T["fb_%d" % c][:], -1024.0, None, A.add), ["fb_%d" % c], ["yfo%d" % c], 0.5)
+            op("Y", 0.1, lambda: g.sync.dma_start(T.yf[:], T.yfo[:]), ["yfo%d" % c for c in range(NC)], ["yf"], sem="o0", x=2.0)
+        for c in range(NC):
+            reduce(t, c)
+            control(t, c)
+            if t < RO - 1:
+                zprep(t + 1, c)
+        if t < RO - 1:
+            zhash(t + 1)
+    plans(RO - 1, RO)
+    V(12, lambda v: v.tensor_scalar(T.Pt[:], T.Al[:], 1024.0, None, A.mult), ["Al"], ["Pt"])
+    V(12, lambda v: v.tensor_tensor(T.ypo[:], T.Pl[:], T.Pt[:], A.add), ["Pl", "Pt"], ["ypo"])
+    op("Y", 0.1, lambda: g.sync.dma_start(T.yp[:], T.ypo[:]), ["ypo"], ["yp"], sem="o1", x=2.0)
+    op("Y", 0.1, lambda: g.sync.dma_start(T.ys[:], T.yso[:]), ["yso%d" % c for c in range(NC)], ["ys"], sem="o2", x=2.0)
+    XF = T["X%d" % (RO % 2)]
+    for c, (lo, hi) in enumerate(CH):
+        bk = "B%d" % (c % 2)
+        P([(T[bk][:, 0:hi - lo], T.WI[:, 128 * k:128 * k + 128], XF[:, 16 * lo + k:16 * hi:16], hi - lo) for k in range(16)],
+          ["WI%d" % k for k in range(16)] + ["X.%d.%d" % (RO % 2, c)], [bk + ".P"])
+        V(hi - lo, lambda v, bk=bk, lo=lo, hi=hi: v.tensor_copy(T.yxo[:, lo:hi], T[bk][:, 0:hi - lo]), [bk + ".P"], ["yxo%d" % c])
+        op("Y", 0.1, lambda lo=lo, hi=hi: g.sync.dma_start(T.yx[:, lo:hi], T.yxo[:, lo:hi]), ["yxo%d" % c], ["yx%d" % c], sem="o%d" % (3 + c), x=2.0)
+
+    engs = ["V", "S", "P", "G", "Y", "N"]
+    order, when = schedule(ops, engs)
+    count = {}
+    done = {}
+    seen = {}
+    for i in order:
+        o = ops[i]
+        e = o["e"]
+        if e != "N":
+            for d, raw in sorted(o["dep"].items()):
+                od = ops[d]
+                if od["e"] == e and not raw and od["sem"] is None:
+                    continue
+                if d not in done:
+                    continue
+                sm, val = done[d]
+                if seen.get((e, sm), 0) < val:
+                    seen[(e, sm)] = val
+                    queue[e].wait_ge(T.sem[sm], val)
+            ins = o["fn"]()
+        if o["sem"] is None:
+            count[e] = count.get(e, 0) + 1
+            ins.then_inc(T.sem[e], 1)
+            done[i] = (e, count[e])
+        elif o["inc"] is None:
+            ins.then_inc(T.sem[o["sem"]], 16)
+            done[i] = (o["sem"], 16)
+            count[o["sem"]] = 16
+        elif e == "G":
+            count["sent"] = count.get("sent", 0) + o["inc"]
+        else:
+            done[i] = (o["sem"], o["inc"])
+            count[o["sem"]] = o["inc"]
+    for sm in sorted(count):
+        if seen.get(("G", sm), 0) < count[sm]:
+            g.wait_ge(T.sem[sm], count[sm])

@@ -2,118 +2,126 @@ from concourse.bass import DstId, RemoteDMATransfer
 from concourse.mybir import AluOpType as A, ActivationFunctionType as F
 
 N, I, W, PLN, RO, B = 4, 192, 3072, 1024, 6, 48
-CH = [(0, 96), (96, 192)]
-NC = len(CH)
-PS = [False, True]
-LV = [True, True]
-PEC = 0.0005
-ZV = 8
+NC, n, m = 2, 96, 6
+ZM = [1, 1, 1, 1]
+ZQ = [(0, 1, "VVVVVVVVVVVVGGGG"), (1, 2, "GGGGGGGGVVVVVVVV"), (2, 4, "VVVVVVVVGGGGSSSS")]
+TO = ["SP", "SP"]
+PG = 4
+HC = True
+DUAL = [0, 0, 0, 0, 0, 1]
+PEC = 0.00044
+VF = 1.05
+LAT = 0.2
+NET = 5.0
+SLACK = 0.05
+PASSES = 4
+STEPS = {"bulk0": 5, "top0": 10, "bulk1": 20, "top1": 30, "write": 40, "rows0": 50, "rows1": 55, "z0": -38, "z1": -40, "z2": 15, "z3": 15, "f0": 8, "f1": 22, "plans": 60}
 OFS = 1536
+EPS = 3.0 / 128
+BO = 2040
+BIG = 262144.0
+RB = RO + 3
 
 SCRATCH = {
     "pli": ("sbuf", [128, PLN], "int32"), "s0i": ("sbuf", [128, I], "int32"), "thi": ("sbuf", [128, I], "int32"),
     "p0i": ("sbuf", [128, 12], "int32"), "f0b": ("sbuf", [128, I], "bfloat16"),
     "X0": ("sbuf", [128, W], "bfloat16"), "X1": ("sbuf", [128, W], "bfloat16"),
     "pid": ("sbuf", [128, 1], "int32"), "pmi": ("sbuf", [128, 1], "int32"), "cols": ("sbuf", [128, 16], "float32"),
-    "iC": ("sbuf", [128, I], "float32"), "iG": ("sbuf", [128, I], "float32"), "iM": ("sbuf", [128, I], "float32"),
-    "iB": ("sbuf", [128, 12], "float32"), "base": ("sbuf", [128, 12], "int32"),
-    "BD": ("sbuf", [128, 128], "bfloat16"), "BD64": ("sbuf", [128, 128], "bfloat16"), "IDb": ("sbuf", [128, 128], "bfloat16"),
-    "half": ("sbuf", [128, 128], "bfloat16"), "ones": ("sbuf", [128, I], "bfloat16"),
-    "LS": ("sbuf", [128, 128], "bfloat16"), "LI": ("sbuf", [128, 128], "bfloat16"), "tmpc": ("sbuf", [128, 128], "bfloat16"),
-    "tmpd": ("sbuf", [128, 128], "bfloat16"), "nIDb": ("sbuf", [128, 128], "bfloat16"), "WD2": ("sbuf", [128, 144], "bfloat16"),
-    "h_0": ("sbuf", [128, 96], "int32"), "Ho_0": ("sbuf", [128, 12], "uint16"), "tmpe": ("sbuf", [128, 128], "bfloat16"),
-    "WD": ("sbuf", [128, 144], "bfloat16"), "WD64": ("sbuf", [128, 144], "bfloat16"), "WD16": ("sbuf", [128, 144], "bfloat16"), "WU": ("sbuf", [128, 144], "bfloat16"),
-    "BDh": ("sbuf", [128, 128], "float16"), "R0h": ("sbuf", [128, 128], "float16"), "E00h": ("sbuf", [128, 128], "float16"),
-    "E0h": ("sbuf", [128, 128], "float16"), "IDh": ("sbuf", [128, 128], "float16"), "nIDh": ("sbuf", [128, 128], "float16"),
-    "ShI": ("sbuf", [128, 128], "float16"), "mk": ("sbuf", [128, I], "float32"), "rsh": ("sbuf", [128, I], "float16"),
-    "rsf": ("sbuf", [128, I], "float32"), "WI": ("sbuf", [128, 16 * 128], "bfloat16"),
-    "C3": ("sbuf", [128, RO * I], "bfloat16"), "phl": ("sbuf", [128, RO * 12], "int32"),
-    "Pl": ("sbuf", [128, 12], "float32"), "Pt": ("sbuf", [128, 12], "float32"), "Pt2": ("sbuf", [128, 12], "float32"),
-    "Al": ("sbuf", [128, 12], "float32"), "ypo": ("sbuf", [128, 12], "float32"), "P0u": ("sbuf", [128, 12], "uint16"),
+    "iC": ("sbuf", [128, 144], "float32"), "iG": ("sbuf", [128, 128], "float32"), "iM": ("sbuf", [128, I], "float32"),
+    "iB": ("sbuf", [128, 36], "int32"), "h": ("sbuf", [128, 96], "int32"), "hf": ("sbuf", [128, 12], "float32"), "hs": ("sbuf", [128, I], "int32"),
+    "Ho": ("sbuf", [128, 12], "uint16"), "P0u": ("sbuf", [128, 12], "uint16"),
+    "WI": ("sbuf", [128, 16 * 128], "bfloat16"), "C3": ("sbuf", [128, RO * I], "bfloat16"), "phl": ("sbuf", [128, RO * 12], "int32"),
+    "Pl": ("sbuf", [128, 3 * RB], "float32"), "Pt": ("sbuf", [128, 12], "float32"), "Pt2": ("sbuf", [128, 12], "float32"),
+    "Al": ("sbuf", [128, 3 * RB], "float32"), "ypo": ("sbuf", [128, 12], "float32"),
     "yso": ("sbuf", [128, I], "float32"), "yfo": ("sbuf", [128, I], "bfloat16"), "yxo": ("sbuf", [128, I], "float32"),
+    "mk": ("sbuf", [128, I], "bfloat16"), "rs": ("sbuf", [128, I], "bfloat16"), "rs1": ("sbuf", [128, I], "bfloat16"),
+    "EH0": ("sbuf", [128, I], "float16"), "EH1": ("sbuf", [128, I], "float16"),
 }
+for _k in ("BD", "IDb", "nIDb", "LS", "LI", "WUB", "tmpc", "tmpe"):
+    SCRATCH[_k] = ("sbuf", [128, 128], "bfloat16")
+for _k in ("WD", "WDn", "WD2", "WD16"):
+    SCRATCH[_k] = ("sbuf", [128, 144], "bfloat16")
+for _k in ("BDh", "R0h", "E00h", "E0h", "IDh", "nIDh", "ID64", "ShI"):
+    SCRATCH[_k] = ("sbuf", [128, 128], "float16")
+for _k, _dt in (("Sh", "float16"), ("eh", "float16"), ("bd", "float16"), ("fb", "float16"), ("So", "uint16"), ("Eo", "uint16")):
+    SCRATCH[_k] = ("sbuf", [128, RB * B], _dt)
+for _k in ("ZR", "dS", "dP", "gS", "aP"):
+    SCRATCH[_k] = ("sbuf", [128, W], "bfloat16")
 for _t in range(RO):
     SCRATCH["Z%d" % _t] = ("sbuf", [128, I], "bfloat16")
     SCRATCH["Y%d" % _t] = ("sbuf", [128, I], "bfloat16")
-for _c, (_a, _b) in enumerate(CH):
-    _n = _b - _a
-    for _nm, _sh, _dt in (("ZR", [16 * _n], "bfloat16"), ("dS", [16 * _n], "bfloat16"), ("dP", [16 * _n], "bfloat16"), ("aS", [16 * _n], "bfloat16"),
-                          ("aP", [16 * _n], "bfloat16"), ("lo", [16 * _n], "bfloat16"), ("E0", [3 * _n], "float16"), ("E1", [3 * _n], "float16"),
-                          ("So", [_n], "uint16"), ("Eo", [_n], "uint16"), ("fb", [_n], "float16"), ("bd", [_n], "float32"),
-                          ("rl", [2 * _n], "bfloat16"), ("hm", [2 * _n], "bfloat16"), ("Wm", [3 * _n], "float16"), ("lb", [_n], "float16"),
-                          ("R", [_n], "float16"), ("tm", [_n], "float16"), ("ts", [_n], "float16"), ("y0", [_n], "float32"), ("v", [_n], "int32"),
-                          ("pm", [_n], "float32"), ("ps", [_n], "int32"), ("pl", [48], "int32"),
-                          ("To", [12], "uint16"), ("Po", [12], "uint16")):
-        SCRATCH["%s_%d" % (_nm, _c)] = ("sbuf", [128] + _sh, _dt)
+for _c in range(NC):
+    for _nm, _sh, _dt in (("rl", 2 * n, "bfloat16"), ("hm", 2 * n, "bfloat16"), ("Wm", 3 * n, "float16"), ("fl", n, "float16"), ("rd", n, "int32"),
+                          ("R", n, "float16"), ("ts", n, "float32"), ("y0", n, "float32"), ("v", n, "int32"),
+                          ("ps", n, "int32"), ("pl", 32, "int32"), ("To", 12, "uint16"), ("Po", 12, "uint16")):
+        SCRATCH["%s_%d" % (_nm, _c)] = ("sbuf", [128, _sh], _dt)
 for _k in range(8):
     SCRATCH["B%d" % _k] = ("psum", [128, 512], "float32")
 
-LOADS = ["x0", "s0", "z0", "pl", "p0", "f0", "th"]
+LOADS = ["x0", "s0", "z0", "z1", "pl", "p0", "f0", "th"]
 SEMAPHORES = ["V", "S", "P", "G", "sent"] + ["ld_" + k for k in LOADS] + ["xc%d" % t for t in range(RO)] + ["o%d" % k for k in range(8)]
-SEMAPHORES += ["a%d_%d" % (t, b) for t in range(RO - 1) for b in range(4) if (b + t) % 4]
+SEMAPHORES += ["a%d_%d" % (t, j) for t in range(RO - 1) for j in range(3)]
 
-CY = 0.00083
-
-
-class _Nothing:
-    pass
+CY = 0.00083 * VF
+ORDER = []
 
 
 def schedule(ops, eng_list):
-    n = len(ops)
-    succ = [[] for _ in range(n)]
+    cnt = len(ops)
+    succ = [[] for _ in range(cnt)]
     for i, o in enumerate(ops):
         for d in o["dep"]:
             succ[d].append(i)
-    lat = 0.08
-    prio = [0.0] * n
-    for i in range(n - 1, -1, -1):
-        m = 0.0
-        for s in succ[i]:
-            x = prio[s] + (lat if ops[s]["e"] != ops[i]["e"] else 0.03)
-            if x > m:
-                m = x
-        prio[i] = m + ops[i]["c"] + ops[i]["x"]
-    left = [len(o["dep"]) for o in ops]
-    ready = {}
-    for e in eng_list:
-        ready[e] = []
-    when = [0.0] * n
-    est = [0.0] * n
-    for i, o in enumerate(ops):
-        if not left[i]:
-            ready[o["e"]].append(i)
-    free = {}
-    for e in eng_list:
-        free[e] = 0.0
-    order = []
-    while len(order) < n:
-        best = None
+    pred = [list(o["dep"]) for o in ops]
+    gap = lambda i, j: 0.0 if ops[i]["e"] == ops[j]["e"] == "P" else LAT
+
+    def run(before, after, prio, back):
+        left = [len(x) for x in before]
+        ready, free = {}, {}
         for e in eng_list:
-            if not ready[e]:
-                continue
-            f = free[e]
-            lowest = min(max(f, est[i]) for i in ready[e])
-            cand = [i for i in ready[e] if max(f, est[i]) <= lowest + 0.02]
-            j = max(cand, key=lambda i: prio[i])
-            k = (max(f, est[j]), -prio[j], j)
-            if best is None or k < best:
-                best = k
-        st, _, j = best
-        o = ops[j]
-        ready[o["e"]].remove(j)
-        order.append(j)
-        if o["e"] != "N":
-            free[o["e"]] = st + o["c"]
-        when[j] = st + o["c"] + o["x"]
-        for s in succ[j]:
-            left[s] -= 1
-            x = when[j] + (lat if ops[s]["e"] != o["e"] else 0.03)
-            if x > est[s]:
-                est[s] = x
-            if not left[s]:
-                ready[ops[s]["e"]].append(s)
-    return order, when
+            ready[e], free[e] = [], 0.0
+        est, end = [0.0] * cnt, [0.0] * cnt
+        for i in range(cnt):
+            if not left[i]:
+                est[i] = ops[i]["x"] if back else 0.0
+                ready[ops[i]["e"]].append(i)
+        order = []
+        while len(order) < cnt:
+            best = None
+            for e in eng_list:
+                if not ready[e]:
+                    continue
+                f = free[e]
+                lowest = max(f, min(est[i] for i in ready[e])) + SLACK
+                j = max((i for i in ready[e] if est[i] <= lowest), key=lambda i: prio[i])
+                k = (max(f, est[j]), -prio[j], j)
+                if best is None or k < best:
+                    best = k
+            st, _, j = best
+            o = ops[j]
+            ready[o["e"]].remove(j)
+            order.append(j)
+            if o["e"] != "N":
+                free[o["e"]] = st + o["c"]
+            end[j] = st + o["c"] + (0.0 if back else o["x"])
+            for s in after[j]:
+                left[s] -= 1
+                x = end[j] + gap(s, j) + (ops[s]["x"] if back else 0.0)
+                if x > est[s]:
+                    est[s] = x
+                if not left[s]:
+                    ready[ops[s]["e"]].append(s)
+        return order, end
+    prio = [0.0] * cnt
+    for i in range(cnt - 1, -1, -1):
+        prio[i] = max([prio[s] for s in succ[i]] + [-ops[i]["ph"] - i / cnt])
+    best = None
+    for _ in range(PASSES):
+        order, end = run(pred, succ, prio, False)
+        if best is None or max(end) < best[0]:
+            best = (max(end), order)
+        prio = run(succ, pred, end, True)[1]
+    return best[1]
 
 
 def rank_program(g, core, T, topo):
@@ -123,6 +131,10 @@ def rank_program(g, core, T, topo):
     ops = []
     last_w, last_r = {}, {}
     banks = {}
+    phase = [0]
+
+    def step(t, name):
+        phase[0] = 100 * t + STEPS[name]
     queue = {"V": g.vector, "S": g.scalar, "P": g.tensor, "G": g, "Y": g.sync, "N": None}
 
     def op(e, c, fn, r=(), w=(), sem=None, x=0.0, inc=None):
@@ -153,45 +165,60 @@ def rank_program(g, core, T, topo):
         for k in w:
             last_w[k] = i
             last_r[k] = []
-        ops.append({"e": e, "c": c, "x": x, "fn": fn, "dep": dep, "sem": sem, "inc": inc})
+        ops.append({"e": e, "c": c, "x": x, "fn": fn, "dep": dep, "sem": sem, "inc": inc, "ph": phase[0]})
         return i
 
-    def V(n, fn, r, w, f=1.0):
-        op("V", max(64, n * f) * CY, lambda: fn(g.vector), r, w)
+    def V(w_, fn, r, w, f=1.0):
+        op("V", max(64, w_ * f) * CY, lambda: fn(g.vector), r, w)
 
-    def VG(n, fn, r, w):
-        op("V", 0.05 + n * 1.5 * CY, lambda: fn(g.vector), r, w)
+    def VG(w_, fn, r, w):
+        op("V", 0.05 + w_ * 1.56 * CY, lambda: fn(g.vector), r, w)
 
-    def S(n, fn, r, w):
-        op("S", 0.06 + n * CY, lambda: fn(g.scalar), r, w)
+    def S(w_, fn, r, w):
+        op("S", 0.06 + w_ * CY, lambda: fn(g.scalar), r, w)
+
+    def copy(e, w_, out, src, r, w):
+        if e == "V":
+            V(w_, lambda v: v.tensor_copy(out, src), r, w, 0.5)
+        elif e == "S":
+            S(w_, lambda s: s.activation(out, src, F.Copy), r, w)
+        else:
+            op("G", 0.19 + 2 * w_ * CY, lambda: g.affine_select(out, src, [[0, w_]], A.is_ge, 0.0, 0, 0), r, w)
 
     def P(mms, r, w, first=True, last=True):
         def fn():
             k = len(mms)
-            for j, (o, l, rr, n) in enumerate(mms):
+            for j, (o, l, rr, _) in enumerate(mms):
                 ins = g.tensor.matmul(o, l, rr, first and j == 0, last and j == k - 1)
             return ins
-        op("P", sum(max(64, m[3]) for m in mms) * PEC, fn, r, w)
+        op("P", sum(max(64, x[3]) for x in mms) * PEC, fn, r, w)
 
-    def load(e, name, dst, w, x):
-        op(e, 0.1, lambda: queue[e].dma_start(dst, T[name][:]), (), w, sem="ld_" + name, x=x)
-    ZK = lambda t: ["Z%d.%d" % (t, b) for b in range(4)]
-    load("Y", "x0", T.X0[:], ["X.0.%d" % c for c in range(NC)], 4.5)
-    load("S", "p0", T.p0i[:], ["p0i"], 2.0)
-    load("S", "pl", T.pli[:], ["pli"], 3.0)
-    load("Y", "s0", T.s0i[:], ["s0i"], 2.5)
-    load("S", "z0", T.Z0[:], ZK(0), 2.2)
-    load("Y", "th", T.thi[:], ["thi"], 2.5)
-    load("S", "f0", T.f0b[:], ["f0b"], 2.2)
+    at = lambda t, j: RO - 1 - t + j
+    cut = lambda buf, p, k=1: buf[:, p * B:(p + k) * B]
+    keys = lambda nm, p, k=1: ["%s.%d" % (nm, q) for q in range(p, p + k)]
+
+    def moves(t, c):
+        if c == 0 or t == RO - 1:
+            return [(0, 2, at(t, 2 * c))]
+        return [(0, 1, at(t, 2)), (B, 1, at(t + 1, 0))]
+
+    def load(e, name, dst, src, w, x):
+        op(e, 0.1, lambda: queue[e].dma_start(dst, src), (), w, sem="ld_" + name, x=x)
+    load("Y", "x0", T.X0[:], T.x0[:], ["X0.0", "X0.1"], 5.0)
+    load("S", "z0", T.Z0[:, 0:3 * B], T.z0[:, B:I], keys("Z0", 0, 3), 2.2)
+    load("S", "s0", T.s0i[:], T.s0[:], ["s0i"], 2.5)
+    load("S", "p0", T.p0i[:], T.p0[:], ["p0i"], 2.0)
+    load("Y", "pl", T.pli[:], T.pl[:], ["pli"], 5.0)
+    load("S", "z1", T.Z0[:, 3 * B:I], T.z0[:, 0:B], keys("Z0", 3), 2.2)
+    load("S", "th", T.thi[:], T.th[:], ["thi"], 2.5)
+    load("S", "f0", T.f0b[:], T.f0[:], ["f0b"], 2.2)
 
     op("G", 0.15, lambda: g.iota(T.pid[:], [[1, 1]], 0, 1), (), ["pid"])
-    op("G", 0.5, lambda: g.iota(T.iC[:], [[1, I]], 0, 0, allow_small_or_imprecise_dtypes=True), (), ["iC"])
-    op("G", 0.5, lambda: g.iota(T.iG[:], [[16, 12], [0, 16]], 0, 0, allow_small_or_imprecise_dtypes=True), (), ["iG"])
+    op("G", 0.4, lambda: g.iota(T.iC[:], [[1, 144]], 0, 0, allow_small_or_imprecise_dtypes=True), (), ["iC"])
+    op("G", 0.4, lambda: g.iota(T.iG[:], [[16, 8], [0, 16]], 0, 0, allow_small_or_imprecise_dtypes=True), (), ["iG"])
     op("G", 0.5, lambda: g.iota(T.iM[:], [[0, 12], [1, 16]], 0, 0, allow_small_or_imprecise_dtypes=True), (), ["iM"])
-    op("G", 0.2, lambda: g.iota(T.iB[:], [[256, 12]], 0, 0, allow_small_or_imprecise_dtypes=True), (), ["iB"])
+    op("G", 0.2, lambda: g.iota(T.iB[:], [[0, 3], [256, 12]], 0, 0), (), ["iB"])
     col = lambda k: T.cols[:, k:k + 1]
-    V(128, lambda v: v.memset(T.half[:], 0.5), (), ["half"])
-    V(192, lambda v: v.memset(T.ones[:], 1.0), (), ["ones"])
     V(1, lambda v: v.tensor_scalar(T.pmi[:], T.pid[:], 15, None, A.bitwise_and), ["pid"], ["pmi"])
     V(1, lambda v: v.tensor_copy(col(0), T.pid[:]), ["pid"], ["c0"])
     V(1, lambda v: v.tensor_copy(col(1), T.pmi[:]), ["pmi"], ["c1"])
@@ -202,300 +229,307 @@ def rank_program(g, core, T, topo):
     V(1, lambda v: v.tensor_scalar(col(6), col(1), 2.0, 1.0, A.mult, A.add), ["c1"], ["c6"])
     V(1, lambda v: v.tensor_scalar(col(7), col(1), 16.0, None, A.mult), ["c1"], ["c7"])
 
-    def cs(out, src, n, c, o0, r, w):
-        V(n, lambda v: v.tensor_scalar(out, src, c, None, o0), r, w)
-    cs(T.WD[:], T.iC[:, 0:144], 144, col(3), A.is_equal, ["iC", "c3"], ["WD"])
-    cs(T.WU[:], T.WD[:], 144, col(6), A.mult, ["WD", "c6"], ["WU"])
-    cs(T.WD64[:], T.WD[:], 72, 1.0 / 64, A.mult, ["WD"], ["WD64"])
-    cs(T.WD16[:], T.WD[:], 72, 1.0 / 16, A.mult, ["WD"], ["WD16"])
-    cs(T.BD[:], T.iG[:, 0:128], 128, col(2), A.is_equal, ["iG", "c2"], ["BD"])
+    def cs(out, src, w_, c, o0, r, w, c2=None, o1=None):
+        if o1 is None:
+            V(w_, lambda v: v.tensor_scalar(out, src, c, None, o0), r, w)
+        else:
+            V(w_, lambda v: v.tensor_scalar(out, src, c, c2, o0, o1), r, w)
+
+    def sc(out, src, w_, c, r, w):
+        cs(out, src, w_ // 2, c, A.mult, r, w)
+    cs(T.WD[:], T.iC[:], 144, col(3), A.is_equal, ["iC", "c3"], ["WD"])
+    sc(T.WDn[:], T.WD[:], 144, -1.0, ["WD"], ["WDn"])
+    sc(T.WD2[:], T.WD[:], 144, -2.0, ["WD"], ["WD2"])
+    sc(T.WD16[:], T.WD[:], 144, 1.0 / 16, ["WD"], ["WD16"])
+    cs(T.BD[:], T.iG[:], 128, col(2), A.is_equal, ["iG", "c2"], ["BD"])
+    sc(T.WUB[:], T.BD[:], 128, col(6), ["BD", "c6"], ["WU"])
     cs(T.IDb[:], T.iC[:, 0:128], 128, col(0), A.is_equal, ["iC", "c0"], ["IDb"])
-    cs(T.mk[:], T.iM[:], 192, col(1), A.is_equal, ["iM", "c1"], ["mk"])
-    cs(T.rsh[:], T.iM[:], 192, 0.0, A.is_gt, ["iM"], ["rsh"])
-    cs(T.rsf[:], T.iM[:], 192, 0.0, A.is_gt, ["iM"], ["rsf"])
+    cs(T.mk[:], T.iM[:], 192, col(1), A.not_equal, ["iM", "c1"], ["mk"], -BIG / 2, A.mult)
+    S(192, lambda s: s.activation(T.rs1[:], T.iM[:], F.Sigmoid, bias=-512.0, scale=1024.0), ["iM"], ["rs1"])
+    cs(T.rs[:], T.rs1[:], 96, 2 * BIG, A.mult, ["rs1"], ["rs"], -BIG, A.add)
     cs(T.tmpc[:], T.iC[:, 0:128], 128, col(0), A.is_gt, ["iC", "c0"], ["tmpc"])
     V(256, lambda v: v.tensor_tensor(T.LS[:], T.tmpc[:], T.BD[:], A.mult), ["tmpc", "BD"], ["LS"])
-    cs(T.tmpd[:], T.IDb[:], 64, 64.0, A.mult, ["IDb"], ["tmpd"])
-    V(256, lambda v: v.tensor_tensor(T.LI[:], T.LS[:], T.tmpd[:], A.subtract), ["LS", "tmpd"], ["LI"])
-    cs(T.IDh[:], T.IDb[:], 64, 1.0, A.mult, ["IDb"], ["IDh"])
-    cs(T.nIDb[:], T.IDb[:], 64, -1.0, A.mult, ["IDb"], ["nIDb"])
-    cs(T.WD2[:], T.WD[:], 72, 2.0, A.mult, ["WD"], ["WD2"])
-    cs(T.nIDh[:], T.IDb[:], 64, -1.0, A.mult, ["IDb"], ["nIDh"])
-    cs(T.BD64[:], T.BD[:], 64, 64.0, A.mult, ["BD"], ["BD64"])
-    cs(T.BDh[:], T.BD[:], 64, 1.0, A.mult, ["BD"], ["BDh"])
-    cs(T.R0h[:], T.BD[:], 64, col(5), A.mult, ["BD", "c5"], ["R0h"])
-    cs(T.E00h[:], T.IDb[:], 64, col(5), A.mult, ["IDb", "c5"], ["E00h"])
-    cs(T.E0h[:], T.WD[:, 15:143], 64, 1.0, A.mult, ["WD"], ["E0h"])
+    V(256, lambda v: v.tensor_tensor(T.LI[:], T.LS[:], T.IDb[:], A.subtract), ["LS", "IDb"], ["LI"])
+    sc(T.IDh[:], T.IDb[:], 128, 1.0, ["IDb"], ["IDh"])
+    if any(ZM):
+        sc(T.nIDb[:], T.IDb[:], 128, -1.0, ["IDb"], ["nIDb"])
+    sc(T.nIDh[:], T.IDb[:], 128, -1.0, ["IDb"], ["nIDh"])
+    sc(T.ID64[:], T.IDb[:], 128, 64.0, ["IDb"], ["ID64"])
+    sc(T.BDh[:], T.BD[:], 128, 1.0, ["BD"], ["BDh"])
+    sc(T.R0h[:], T.BD[:], 128, col(5), ["BD", "c5"], ["R0h"])
+    sc(T.E00h[:], T.IDb[:], 128, col(5), ["IDb", "c5"], ["E00h"])
+    sc(T.E0h[:], T.WD[:, 15:143], 128, 1.0, ["WD"], ["E0h"])
     cs(T.tmpe[:], T.iC[:, 0:128], 128, col(4), A.is_equal, ["iC", "c4"], ["tmpe"])
-    V(256, lambda v: v.tensor_tensor(T.tmpe[:], T.tmpe[:], T.BD[:], A.mult), ["tmpe", "BD"], ["tmpe"])
-    V(256, lambda v: v.tensor_tensor(T.ShI[:], T.tmpe[:], T.IDb[:], A.subtract), ["tmpe", "IDb"], ["ShI"])
-    cs(T.base[:], T.iB[:], 12, col(7), A.add, ["iB", "c7"], ["base"])
+    V(256, lambda v: v.tensor_tensor(T.tmpc[:], T.tmpe[:], T.BD[:], A.mult), ["tmpe", "BD"], ["tmpc"])
+    V(256, lambda v: v.tensor_tensor(T.ShI[:], T.tmpc[:], T.IDb[:], A.subtract), ["tmpc", "IDb"], ["ShI"])
 
-    V(12, lambda v: v.tensor_copy(T.P0u[:], T.p0i[:]), ["p0i"], ["P0u"])
-    V(12, lambda v: v.tensor_copy(T.Pl[:], T.p0i[:]), ["p0i"], ["Pl"])
-    for c, (lo, hi) in enumerate(CH):
-        n = hi - lo
-        b = lambda nm, c=c: T["%s_%d" % (nm, c)]
-        K = lambda nm, c=c: "%s_%d" % (nm, c)
-        V(n, lambda v, b=b, lo=lo, hi=hi: v.tensor_copy(b("So")[:], T.s0i[:, lo:hi]), ["s0i"], [K("So")])
-        V(n, lambda v, b=b, lo=lo, hi=hi, n=n: v.tensor_scalar(b("E0")[:, 2 * n:3 * n], T.s0i[:, lo:hi], -float(OFS), None, A.add), ["s0i"], [K("S0")])
-        if lo % 32 == 0:
-            pu, pk = (lambda lo=lo, hi=hi: T.P0u[:, lo // 16:hi // 16]), "P0u"
-        else:
-            V(n, lambda v, b=b, lo=lo, hi=hi: v.tensor_copy(b("Po")[:, 0:(hi - lo) // 16], T.p0i[:, lo // 16:hi // 16]), ["p0i"], [K("Po")])
-            pu, pk = (lambda b=b, n=n: b("Po")[:, 0:n // 16]), K("Po")
-        VG(n, lambda v, b=b, n=n, pu=pu: v.tensor_scalar(b("E0")[:, n:2 * n], T.pli[:, :].indirect(pu()), -float(OFS), None, A.add), ["pli", pk], [K("e0")])
-        V(n, lambda v, b=b, n=n: v.tensor_scalar(b("Eo")[:], b("E0")[:, n:2 * n], float(OFS), None, A.add), [K("e0")], [K("Eo")], 0.5)
-        V(n, lambda v, b=b, lo=lo, hi=hi: v.tensor_scalar(b("fb")[:], T.f0b[:, lo:hi], 1024.0, None, A.add), ["f0b"], [K("fb")], 0.5)
-        V(n, lambda v, b=b, lo=lo, hi=hi: v.tensor_scalar(b("bd")[:], T.thi[:, lo:hi], 1.0 / 64, None, A.mult), ["thi"], [K("bd")])
+    for j, k, b0 in ((0, 3, 1), (3, 1, 0)):
+        p, w_ = at(0, j), k * B
+        V(12, lambda v, j=j, k=k, b0=b0: v.tensor_copy(T.P0u[:, 3 * j:3 * (j + k)], T.p0i[:, 3 * b0:3 * (b0 + k)]), ["p0i"], ["P0u.%d" % j])
+        V(12, lambda v, p=p, k=k, b0=b0: v.tensor_copy(T.Pl[:, 3 * p:3 * (p + k)], T.p0i[:, 3 * b0:3 * (b0 + k)]), ["p0i"], ["Pl"])
+        V(w_, lambda v, p=p, k=k, b0=b0: v.tensor_copy(cut(T.So, p, k), cut(T.s0i, b0, k)), ["s0i"], keys("So", p, k))
+        cs(cut(T.Sh, p, k), cut(T.s0i, b0, k), w_, -float(OFS), A.add, ["s0i"], keys("Sh", p, k))
+        cs(cut(T.fb, p, k), cut(T.f0b, b0, k), w_ // 2, 1024.0, A.add, ["f0b"], keys("fb", p, k))
+        cs(cut(T.bd, p, k), cut(T.thi, b0, k), w_, -float(BO), A.add, ["thi"], keys("bd", p, k))
+    for c in range(NC):
+        p = at(0, 2 * c)
+        VG(n, lambda v, c=c, p=p: v.tensor_scalar(cut(T.eh, p, 2), T.pli[:, :].indirect(T.P0u[:, m * c:m * c + m]), -float(OFS), None, A.add), ["pli", "P0u.0", "P0u.3"], keys("eh", p, 2))
+        cs(cut(T.Eo, p, 2), cut(T.eh, p, 2), n // 2, float(OFS), A.add, keys("eh", p, 2), keys("Eo", p, 2))
 
     win = lambda nm, k: T[nm][:, 15 - k:143 - k]
+    subs = [0]
+    xat = [sum(DUAL[:t]) % 2 for t in range(RO + 1)]
 
     def zprep(t, c):
-        lo, hi = CH[c]
-        n, m = hi - lo, (hi - lo) // 16
-        b = lambda nm: T["%s_%d" % (nm, c)]
-        K = lambda nm: "%s_%d" % (nm, c)
-        Z = T["Z%d" % t]
-        zk = ["Z%d.%d" % (t, k) for k in range(lo // B, hi // B)]
-        for k in range(16):
-            if k < ZV:
-                V(n, lambda v, k=k: v.tensor_copy(b("ZR")[:, k:16 * n:16], Z[:, lo:hi]), zk, [K("ZR") + ".%d" % k], 0.5)
-            else:
-                S(n, lambda s, k=k: s.activation(b("ZR")[:, k:16 * n:16], Z[:, lo:hi], F.Copy), zk, [K("ZR") + ".%d" % k])
-        P([(T.B7[:, 0:n], T.IDh[:], b("fb")[:], n), (T.B7[:, 0:n], T.IDb[:], Z[:, lo:hi], n)], [K("fb"), "IDh", "IDb"] + zk, ["B7.f"])
-        V(n, lambda v: v.tensor_scalar(b("fb")[:], T.B7[:, 0:n], 0.5, 511.75, A.mult, A.add), ["B7.f"], [K("fb")])
+        Z, zn = T["Z%d" % t], "Z%d" % t
+        for j0, j1, qs in ZQ:
+            if j0 // 2 == c:
+                step(t, "z%d" % j0)
+                for k in range(16):
+                    copy(qs[k], (j1 - j0) * B, T.ZR[:, 16 * B * j0 + k:16 * B * j1:16], cut(Z, j0, j1 - j0), keys(zn, j0, j1 - j0), ["ZR.%d.%d" % (j, k) for j in range(j0, j1)])
+        p = at(t, 2 * c)
+        step(t, "f%d" % c)
+        if c == 0 and t:
+            old, ok = [(T.B7[:, 0:B], T.IDh[:], cut(T.fb, p + 4), B), (T.B7[:, B:n], T.IDh[:], cut(T.fb, p + 1), B)], keys("fb", p + 4) + keys("fb", p + 1)
+        else:
+            old, ok = [(T.B7[:, 0:n], T.IDh[:], cut(T.fb, p, 2), n)], keys("fb", p, 2)
+        P([(T.B7[:, 0:n], T.IDb[:], cut(Z, 2 * c, 2), n)] + old, ok + ["IDh", "IDb"] + keys(zn, 2 * c, 2), ["B7.f"])
+        V(n, lambda v: v.tensor_scalar(cut(T.fb, p, 2), T.B7[:, 0:n], 0.5, 511.75, A.mult, A.add), ["B7.f"], keys("fb", p, 2))
 
-    def zhash(t):
-        m = 12
+    def zhash(t, c0, c1):
         Z = T["Z%d" % t]
-        P([(T.B7[:, 256:256 + m], win("WU", k), Z[:, k:I:16], m) for k in range(16)], ["WU"] + ZK(t), ["B7.u"])
-        h = lambda k: T.h_0[:, 12 * k:12 * k + m]
-        H = lambda k: "h.%d" % k
-        ph = T.phl[:, 12 * t:12 * t + 12]
-        V(m, lambda v: v.tensor_copy(h(0), T.B7[:, 256:256 + m]), ["B7.u"], [H(0)])
-        V(m, lambda v: v.tensor_scalar(h(1), h(0), 4095, None, A.bitwise_and), [H(0)], [H(1)])
-        V(m, lambda v: v.tensor_tensor(h(2), h(1), h(1), A.mult), [H(1)], [H(2)])
-        V(m, lambda v: v.tensor_scalar(h(4), h(1), 37.0, None, A.mult), [H(1)], [H(4)])
-        V(m, lambda v: v.tensor_scalar(h(3), h(2), 5, None, A.logical_shift_right), [H(2)], [H(3)])
-        V(m, lambda v: v.tensor_tensor(h(5), h(3), h(4), A.add), [H(3), H(4)], [H(5)])
-        V(m, lambda v: v.tensor_scalar(ph, h(5), 1023, None, A.bitwise_and), [H(5)], ["ph%d" % t])
-        V(m, lambda v: v.tensor_copy(T.Ho_0[:], ph), ["ph%d" % t], ["Ho"])
-        for c, (lo, hi) in enumerate(CH):
-            VG(hi - lo, lambda v, c=c, lo=lo, hi=hi: v.tensor_scalar(T["E%d_%d" % (t % 2, c)][:, 0:hi - lo], T.pli[:, :].indirect(T.Ho_0[:, lo // 16:hi // 16]), -float(OFS), None, A.add),
-               ["pli", "Ho"], ["eh%d_%d" % (t % 2, c)])
+        lo, hi = c0 * n, c1 * n
+        h = lambda k: T.h[:, 12 * k + m * c0:12 * k + m * c1]
+        H = lambda k: "h.%d.%d" % (k, c0)
+        ph, hf = T.phl[:, 12 * t + m * c0:12 * t + m * c1], T.hf[:, m * c0:m * c1]
+        u = T.B7[:, 256 + lo:256 + hi]
+        P([(u, T.IDb[:], T.mk[:, lo:hi], hi - lo), (u, T.WUB[:], Z[:, lo:hi], hi - lo)], ["WU", "mk", "IDb"] + keys("Z%d" % t, 2 * c0, 2 * (c1 - c0)), ["B7.u"])
+        V(hi - lo, lambda v: v.tensor_tensor_scan(T.hs[:, lo:hi], T.rs[:, lo:hi], u, 0.0, A.min, A.max), ["B7.u", "rs"], [H(0)])
+        V(m, lambda v: v.tensor_scalar(h(1), T.hs[:, lo + 15:hi:16], 4095, None, A.bitwise_and), [H(0)], [H(1)])
+        V(m, lambda v: v.tensor_scalar(hf, h(1), 1184.0, None, A.add), [H(1)], [H(2)])
+        V(m, lambda v: v.tensor_tensor(h(3), h(1), hf, A.mult), [H(1), H(2)], [H(3)])
+        V(m, lambda v: v.tensor_scalar(ph, h(3), 5, 1023, A.logical_shift_right, A.bitwise_and), [H(3)], keys("ph%d" % t, c0, c1 - c0))
+        V(m, lambda v: v.tensor_copy(T.Ho[:, m * c0:m * c1], ph), keys("ph%d" % t, c0, c1 - c0), keys("Ho", c0, c1 - c0))
+        VG(hi - lo, lambda v: v.tensor_scalar(T["EH%d" % (t % 2)][:, lo:hi], T.pli[:, :].indirect(T.Ho[:, m * c0:m * c1]), -float(OFS), 1.0 / 64, A.add, A.mult),
+           ["pli"] + keys("Ho", c0, c1 - c0), keys("EH%d" % (t % 2), c0, c1 - c0))
 
     def bulk(t, c):
-        lo, hi = CH[c]
-        n = hi - lo
-        b = lambda nm: T["%s_%d" % (nm, c)]
-        K = lambda nm: "%s_%d" % (nm, c)
-        X = T["X%d" % (t % 2)]
-        xk = ["X.%d.%d" % (t % 2, k) for k in range(NC)]
-        ks = range(lo // B, hi // B)
-        for dst, of in (("dS", "So"), ("dP", "Eo")):
-            for k in ks:
-                u = k * B - lo
-                if dst == "dP" and PS[c]:
-                    op("S", 0.065 + 16 * B * 1.5 * CY, lambda dst=dst, of=of, u=u: g.scalar.activation(b(dst)[:, 16 * u:16 * (u + B)], X[:, :].indirect(b(of)[:, u:u + B]), F.Copy),
-                       xk + [K(of)], [K(dst) + ".%d" % k])
-                    continue
-                VG(16 * B, lambda v, dst=dst, of=of, u=u: v.tensor_tensor(b(dst)[:, 16 * u:16 * (u + B)], X[:, :].indirect(b(of)[:, u:u + B]), b("ZR")[:, 16 * u:16 * (u + B)], A.subtract),
-                   xk + [K(of)] + [K("ZR") + ".%d" % j for j in range(16)], [K(dst) + ".%d" % k])
-        for k in ks:
-            sl = slice(16 * (k * B - lo), 16 * (k * B - lo + B))
-            S(16 * B, lambda s, sl=sl: s.activation(b("aS")[:, sl], b("dS")[:, sl], F.Abs), [K("dS") + ".%d" % k], [K("aS") + ".%d" % k])
-            if not PS[c]:
-                S(16 * B, lambda s, sl=sl: s.activation(b("aP")[:, sl], b("dP")[:, sl], F.Abs), [K("dP") + ".%d" % k], [K("aP") + ".%d" % k])
-            if LV[c]:
-                V(16 * B, lambda v, sl=sl: v.tensor_scalar(b("lo")[:, sl], b("dS")[:, sl], 0.0, None, A.is_le), [K("dS") + ".%d" % k], [K("lo") + ".%d" % k], 0.5)
-            else:
-                S(16 * B, lambda s, sl=sl: s.activation(b("lo")[:, sl], b("dS")[:, sl], F.Sign, bias=0.5, scale=-1.0), [K("dS") + ".%d" % k], [K("lo") + ".%d" % k])
-        if PS[c]:
-            Z = T["Z%d" % t]
-            zk = ["Z%d.%d" % (t, k) for k in ks]
-            for j in range(4):
-                bn = "B%d" % (1 + j % 2)
-                d = T[bn]
-
-                def sub(j=j, d=d):
-                    for q in range(4):
-                        g.tensor.matmul(d[:, q * n:q * n + n], T.IDb[:], b("dP")[:, 4 * j + q:16 * n:16], True, False)
-                        ins = g.tensor.matmul(d[:, q * n:q * n + n], T.nIDb[:], Z[:, lo:hi], False, True)
-                    return ins
-                op("P", 8 * n * PEC, sub, ["IDb", "nIDb"] + zk + [K("dP") + ".%d" % k for k in ks], [bn + ".d"])
-                S(4 * n, lambda s, j=j, d=d: s.activation(b("aP")[:, 4 * j * n:4 * (j + 1) * n], d[:, 0:4 * n], F.Abs), [bn + ".d"], [K("aP") + ".j%d" % j])
+        step(t, "bulk%d" % c)
+        X = T["X%d" % xat[t]]
+        xk = keys("X%d" % xat[t], 0, 2)
+        for j in (2 * c, 2 * c + 1):
+            sl = slice(16 * B * j, 16 * B * (j + 1))
+            zr = ["ZR.%d.%d" % (j, k) for k in range(16)]
+            p = at(t, j)
+            VG(16 * B, lambda v, sl=sl, p=p: v.tensor_tensor(T.dS[:, sl], X[:, :].indirect(cut(T.So, p)), T.ZR[:, sl], A.subtract), xk + keys("So", p) + zr, keys("dS", j))
+            V(16 * B, lambda v, sl=sl: v.tensor_scalar(T.gS[:, sl], T.dS[:, sl], EPS, None, A.max), keys("dS", j), keys("gS", j), 0.5)
+            if not ZM[j]:
+                VG(16 * B, lambda v, sl=sl, p=p: v.tensor_tensor(T.dP[:, sl], X[:, :].indirect(cut(T.Eo, p)), T.ZR[:, sl], A.subtract), xk + keys("Eo", p) + zr, keys("dP", j))
+                S(16 * B, lambda s, sl=sl: s.activation(T.aP[:, sl], T.dP[:, sl], F.Abs), keys("dP", j), keys("aP", 2 * j, 2))
+                continue
+            op("S", 0.065 + 16 * B * 1.56 * CY, lambda sl=sl, p=p: g.scalar.activation(T.dP[:, sl], X[:, :].indirect(cut(T.Eo, p)), F.Copy), xk + keys("Eo", p), keys("dP", j))
+            for q in range(2):
+                bn = "B%d" % (2 + subs[0] % 2)
+                subs[0] += 1
+                sl = slice(8 * B * (2 * j + q), 8 * B * (2 * j + q + 1))
+                P([(T[bn][:, 0:8 * B], T.nIDb[:], T.ZR[:, sl], 8 * B), (T[bn][:, 0:8 * B], T.IDb[:], T.dP[:, sl], 8 * B)], ["IDb", "nIDb"] + keys("dP", j) + zr, [bn + ".d"])
+                S(8 * B, lambda s, sl=sl, bn=bn: s.activation(T.aP[:, sl], T[bn][:, 0:8 * B], F.Abs), [bn + ".d"], keys("aP", 2 * j + q))
 
     def reduce(t, c):
-        lo, hi = CH[c]
-        n = hi - lo
-        b = lambda nm: T["%s_%d" % (nm, c)]
-        K = lambda nm: "%s_%d" % (nm, c)
-        q = lambda nm: [K(nm) + ".%d" % k for k in range(lo // B, hi // B)]
-        P([(T.B0[:, n:2 * n], win("WD64", k), b("aS")[:, k:16 * n:16], n) for k in range(16)], ["WD64"] + q("aS"), ["B0.S"])
-        if PS[c]:
-            for j in range(4):
-                P([(T.B0[:, 0:n], win("WD64", k), b("aP")[:, k * n:k * n + n], n) for k in range(4 * j, 4 * j + 4)], ["WD64", K("aP") + ".j%d" % j, "B0.P" if j else "B0.S"], ["B0.P"],
-                  first=j == 0, last=j == 3)
-        else:
-            P([(T.B0[:, 0:n], win("WD64", k), b("aP")[:, k:16 * n:16], n) for k in range(16)], ["WD64"] + q("aP"), ["B0.P"])
+        step(t, "bulk%d" % c)
+        bk = "B%d" % c
+        D = T[bk]
+        p = at(t, 2 * c)
+        groups = {"S": (D[:, n:2 * n], [("WD", "dS", keys("dS", 2 * c, 2)), ("WD2", "gS", keys("gS", 2 * c, 2))]), "P": (D[:, 0:n], [("WDn", "aP", keys("aP", 4 * c, 4))])}
+        for nm in TO[c]:
+            out, streams = groups[nm]
+            P([(out, T.IDh[:], cut(T.bd, p, 2), n)], ["IDh"] + keys("bd", p, 2), [bk + "." + nm, bk + ".open"], last=False)
+            for j, (wn, src, ks) in enumerate(streams):
+                for k0 in range(0, 16, PG):
+                    P([(out, win(wn, k), T[src][:, 16 * n * c + k:16 * n * (c + 1):16], n) for k in range(k0, k0 + PG)], [wn] + ks, [bk + "." + nm, bk + ".open"],
+                      first=False, last=j == len(streams) - 1 and k0 + PG == 16)
 
     def control(t, c):
-        lo, hi = CH[c]
-        n, m = hi - lo, (hi - lo) // 16
+        lo, hi = c * n, c * n + n
         b = lambda nm: T["%s_%d" % (nm, c)]
         K = lambda nm: "%s_%d" % (nm, c)
-        par, nxt = t % 2, (t + 1) % 2
-        E, En = b("E%d" % par), b("E%d" % nxt)
-        kS, ke, keh = K("S%d" % par), K("e%d" % par), K("eh%d" % par)
-        X, Xn = T["X%d" % par], T["X%d" % nxt]
-        xk = ["X.%d.%d" % (par, k) for k in range(NC)]
+        p = at(t, 2 * c)
+        Sh, e, EH = cut(T.Sh, p, 2), cut(T.eh, p, 2), T["EH%d" % (t % 2)][:, lo:hi]
+        kS, ke, kH = keys("Sh", p, 2), keys("eh", p, 2), keys("EH%d" % (t % 2), c)
+        X, Xn = T["X%d" % xat[t]], T["X%d" % xat[t + 1]]
+        xk = keys("X%d" % xat[t], 0, 2)
         Z, Y = T["Z%d" % t], T["Y%d" % t]
-        zk = ["Z%d.%d" % (t, k) for k in range(lo // B, hi // B)]
-        bk = "B0"
+        zk, yk = keys("Z%d" % t, 2 * c, 2), keys("Y%d" % t, 2 * c, 2)
+        bk = "B%d" % c
         D = T[bk]
         last = t == RO - 1
-        P([(T.B6[:, 0:n], T.IDh[:], E[:, n:2 * n], n), (T.B6[:, 0:n], T.nIDh[:], E[:, 2 * n:3 * n], n)], [kS, ke, "IDh", "nIDh"], ["B6.d"])
+        C, U, Q = T.B4, T.B5, T.B6
+        step(t, "rows%d" % c)
+        P([(U[:, 0:n], T.IDh[:], e, n), (U[:, 0:n], T.nIDh[:], Sh, n)], kS + ke + ["IDh", "nIDh"], ["B5.d"])
         if not last:
-            P([(T.B6[:, n:2 * n], T.IDh[:], E[:, 0:n], n), (T.B6[:, n:2 * n], T.nIDh[:], E[:, n:2 * n], n)], [keh, ke, "IDh", "nIDh"], ["B6.e"])
+            P([(U[:, n:2 * n], T.ID64[:], EH, n), (U[:, n:2 * n], T.nIDh[:], e, n)], kH + ke + ["ID64", "nIDh"], ["B5.e"])
+        step(t, "top%d" % c)
         rl = b("rl")
-        V(n, lambda v: v.tensor_tensor(rl[:, n:2 * n], D[:, n:2 * n], b("bd")[:], A.is_lt), [bk + ".S", K("bd")], [K("rS")])
-        V(n, lambda v: v.tensor_tensor(rl[:, 0:n], D[:, 0:n], b("bd")[:], A.is_lt), [bk + ".P", K("bd")], [K("rP")])
-        B3 = T.B3
-        rr = [K("rS"), K("rP")]
-        P([(B3[:, n:3 * n], T.half[:], T.ones[:, 0:2 * n], 2 * n), (B3[:, n:3 * n], T.LI[:], rl[:, 0:2 * n], 2 * n), (B3[:, n:2 * n], T.BD[:], rl[:, n:2 * n], n)],
-          rr + ["half", "ones", "LI", "BD"], ["B3.h"])
-        P([(B3[:, 0:n], T.BD[:], rl[:, n:2 * n], n), (B3[:, 0:n], T.BD[:], rl[:, 0:n], n)], rr + ["BD"], ["B3.t"])
-        P([(B3[:, 3 * n:4 * n], T.LS[:], rl[:, n:2 * n], n)], [K("rS"), "LS"], ["B3.m"])
-        S(3 * n, lambda s: s.activation(T.B4[:, 0:3 * n], B3[:, 0:3 * n], F.Relu, bias=1.0, scale=-1.0), ["B3.h", "B3.t"], ["B4.h"])
-        S(2 * n, lambda s: s.activation(b("hm")[:], B3[:, 2 * n:4 * n], F.Relu, bias=1.0, scale=-1.0), ["B3.h", "B3.m"], [K("hm")])
-        c3 = T.C3[:, t * I + lo:t * I + hi]
-        S(n, lambda s: s.activation(c3, B3[:, 0:n], F.Relu, bias=1.0, scale=-1.0), ["B3.t"], ["C3_%d_%d" % (t, c)])
+        S(2 * n, lambda s: s.activation(rl[:], D[:, 0:2 * n], F.Sigmoid, bias=(BO - 0.125) * 1024, scale=1024.0), [bk + ".S", bk + ".P"], [K("rl")])
+        rP, rS = rl[:, 0:n], rl[:, n:2 * n]
+        P([(C[:, n:3 * n], T.LI[:], rl[:], 2 * n), (C[:, n:2 * n], T.BD[:], rS, n)], [K("rl"), "LI", "BD"], ["B4.h"])
+        P([(C[:, 0:n], T.BD[:], rS, n), (C[:, 0:n], T.BD[:], rP, n)], [K("rl"), "BD"], ["B4.t"])
+        P([(C[:, 3 * n:4 * n], T.LS[:], rS, n)], [K("rl"), "LS"], ["B4.m"])
+        P([(C[:, 4 * n:5 * n], T.BD[:], rS, n)], [K("rl"), "BD"], ["B4.c"])
+        S(2 * n, lambda s: s.activation(C[:, n:3 * n], C[:, n:3 * n], F.Relu, scale=-1.0), ["B4.h"], ["B4.h"])
+        S(n, lambda s: s.activation(C[:, 0:n], C[:, 0:n], F.Relu, bias=64.0, scale=-64.0), ["B4.t"], ["B4.t"])
         Wm = b("Wm")
-        V(3 * n, lambda v: v.tensor_tensor(Wm[:], E[:], T.B4[:, 0:3 * n], A.mult), [kS, ke, keh, "B4.h"], [K("Wm")])
-        P([(T.B5[:, 0:n], T.R0h[:], Wm[:, 0:n], n), (T.B5[:, 0:n], T.BDh[:], Wm[:, n:2 * n], n), (T.B5[:, 0:n], T.BDh[:], Wm[:, 2 * n:3 * n], n)],
-          [K("Wm"), "R0h", "BDh"], ["B5.t"])
-        V(n, lambda v: v.tensor_tensor(b("tm")[:], T.B5[:, 0:n], T.mk[:, 0:n], A.mult), ["B5.t", "mk"], [K("tm")])
-        V(n, lambda v: v.tensor_tensor_scan(b("ts")[:], T.rsh[:, 0:n], b("tm")[:], 0.0, A.mult, A.add), [K("tm"), "rsh"], [K("ts")], 0.5)
+        for q, (src, ks) in enumerate(((EH, kH + ["B4.t"]), (e, ke + ["B4.h"]), (Sh, kS + ["B4.h"]))):
+            V(n, lambda v, q=q, src=src: v.tensor_tensor(Wm[:, q * n:q * n + n], src, C[:, q * n:q * n + n], A.mult), ks, [K("Wm%d" % q)])
+        wk = [K("Wm%d" % q) for q in range(3)]
+        step(t, "rows%d" % c)
+        if not last:
+            for u, k, d in moves(t, c):
+                V(k * B, lambda v, u=u, k=k, d=d: v.tensor_tensor(cut(T.bd, d, k), cut(T.bd, p + u // B, k), C[:, u:u + k * B], A.add), ["B4.t"] + keys("bd", p + u // B, k), keys("bd", d, k))
+        hm = b("hm")
+        S(2 * n, lambda s: s.activation(hm[:], C[:, 3 * n:5 * n], F.Relu, bias=1.0, scale=-1.0), ["B4.m", "B4.c"], [K("hm")])
+        c3 = T.C3[:, t * I + lo:t * I + hi]
+        S(n, lambda s: s.activation(c3, C[:, 0:n], F.Copy, scale=1.0 / 64), ["B4.t"], ["C3_%d_%d" % (t, c)])
+        step(t, "top%d" % c)
+        P([(Q[:, 0:n], T.IDb[:], T.mk[:, 0:n], n), (Q[:, 0:n], T.R0h[:], Wm[:, 0:n], n), (Q[:, 0:n], T.BDh[:], Wm[:, n:2 * n], n), (Q[:, 0:n], T.BDh[:], Wm[:, 2 * n:3 * n], n)],
+          wk + ["R0h", "BDh", "mk", "IDb"], ["B6.t"])
+        V(n, lambda v: v.tensor_tensor_scan(b("ts")[:], T.rs[:, 0:n], Q[:, 0:n], 0.0, A.min, A.max), ["B6.t", "rs"], [K("ts")])
         V(m, lambda v: v.tensor_scalar(b("To")[:, 0:m], b("ts")[:, 15:n:16], float(OFS), None, A.add), [K("ts")], [K("To")])
-        VG(n, lambda v: v.tensor_tensor(b("y0")[:], X[:, :].indirect(b("To")[:, 0:m]), b("fb")[:], A.subtract), xk + [K("To"), K("fb")], [K("y0")])
-        yk = ["Y%d.%d" % (t, k) for k in range(lo // B, hi // B)]
+        VG(n, lambda v: v.tensor_tensor(b("y0")[:], X[:, :].indirect(b("To")[:, 0:m]), cut(T.fb, p, 2), A.subtract), xk + [K("To")] + keys("fb", p, 2), [K("y0")])
         S(n, lambda s: s.activation(Y[:, lo:hi], b("y0")[:], F.Abs, bias=1024.0), [K("y0")], yk)
         if not last:
-            go = [k for k in range(lo // B, hi // B) if (k + t) % 4]
-            stay = [k for k in range(lo // B, hi // B) if (k + t) % 4 == 0]
-            for k in stay:
-                V(B, lambda v, k=k: v.tensor_copy(T["Z%d" % (t + 1)][:, k * B:k * B + B], Y[:, k * B:k * B + B]), ["Y%d.%d" % (t, k)], ["Z%d.%d" % (t + 1, k)])
-            cnt = 8 // len(go) if len(go) in (1, 2) else 2
+            Zn = T["Z%d" % (t + 1)]
+            go = [j for j in (2 * c, 2 * c + 1) if j < 3]
+            per = 8 // len(go)
 
             def send():
                 tr = []
-                for q, k in enumerate(go):
-                    dst = T.cores[(rank + k + t) % N]
+                for q, j in enumerate(go):
+                    dst = T.cores[(rank + at(t, j) % 4 + t) % N]
                     rid, pc = topo.addr(dst, core)
-                    es = topo.engines(core, dst)[q * cnt:(q + 1) * cnt]
-                    tr.append(RemoteDMATransfer(dst_ids=[DstId(rid=rid, pnc=pc)], dma_engine_mask=sum(1 << x for x in es), remote_sem=T.sem["a%d_%d" % (t, k)],
-                                                src=Y[:, k * B:k * B + B], dst=T["Z%d" % (t + 1)][:, k * B:k * B + B]))
+                    es = topo.engines(core, dst)[q * per:(q + 1) * per]
+                    tr.append(RemoteDMATransfer(dst_ids=[DstId(rid=rid, pnc=pc)], dma_engine_mask=sum(1 << x for x in es), remote_sem=T.sem["a%d_%d" % (t, j)],
+                                                src=cut(Y, j), dst=cut(Zn, j + 1)))
                 g.remote_dma_fused(tr, local_sem=T.sem.sent)
-            op("G", 1.0, send, ["Y%d.%d" % (t, k) for k in go], ["net"], sem="sent", inc=cnt * len(go))
-            for k in go:
-                op("N", 0.0, None, ["net"], ["Z%d.%d" % (t + 1, k)], sem="a%d_%d" % (t, k), inc=cnt, x=3.0)
-        P([(T.B5[:, n:2 * n], T.BD[:], Y[:, lo:hi], n)], yk + ["BD"], ["B5.y"])
-        V(n, lambda v: v.tensor_tensor(b("pm")[:], T.B5[:, n:2 * n], T.mk[:, 0:n], A.mult), ["B5.y", "mk"], [K("pm")])
-        V(n, lambda v: v.tensor_tensor_scan(b("ps")[:], T.rsf[:, 0:n], b("pm")[:], 0.0, A.mult, A.add), [K("pm"), "rsf"], [K("ps")])
-        p = lambda k: b("pl")[:, 12 * k:12 * k + m]
-        V(m, lambda v: v.tensor_scalar(p(0), b("ps")[:, 15:n:16], 15, None, A.bitwise_and), [K("ps")], [K("p0")])
-        V(m, lambda v: v.tensor_tensor(p(1), p(0), T.base[:, lo // 16:hi // 16], A.add), [K("p0"), "base"], [K("p1")])
-        V(m, lambda v: v.tensor_copy(b("Po")[:, 0:m], p(1)), [K("p1")], [K("Po")])
-        hm = b("hm")
-        lw = "WD2" if LV[c] else "WD"
-        P([(T.B0[:, 2 * n:3 * n], T.BD64[:], hm[:, 0:n], n)] + [(T.B0[:, 2 * n:3 * n], win(lw, k), b("lo")[:, k:16 * n:16], n) for k in range(16)],
-          [K("hm"), "BD64", lw] + [K("lo") + ".%d" % k for k in range(lo // B, hi // B)], ["B0.l"])
-        V(n, lambda v: v.tensor_scalar(b("lb")[:], T.B0[:, 2 * n:3 * n], 86.0 if LV[c] else 70.0, None, A.is_ge), ["B0.l"], [K("lb")])
-        V(n, lambda v: v.tensor_tensor(T.B6[:, 0:n], T.B6[:, 0:n], b("lb")[:], A.mult), ["B6.d", K("lb")], ["B6.d"])
-        V(n, lambda v: v.tensor_tensor(b("R")[:], E[:, 2 * n:3 * n], T.B6[:, 0:n], A.add), ["B6.d", kS], [K("R")])
+            op("G", 0.7, send, [k for j in go for k in keys("Y%d" % t, j)], [K("net%d" % t)], sem="sent", inc=per * len(go))
+            for j in go:
+                op("N", 0.0, None, [K("net%d" % t)], keys("Z%d" % (t + 1), j + 1), sem="a%d_%d" % (t, j), inc=per, x=NET)
+            if c == 1:
+                S(B, lambda s: s.activation(cut(Zn, 0), b("y0")[:, B:n], F.Abs, bias=1024.0), [K("y0")], keys("Z%d" % (t + 1), 0))
+        P([(Q[:, n:2 * n], T.IDb[:], T.mk[:, 0:n], n), (Q[:, n:2 * n], T.BD[:], Y[:, lo:hi], n)], yk + ["BD", "mk", "IDb"], ["B6.y"])
+        P([(Q[:, 2 * n:3 * n], T.IDb[:], Z[:, lo:hi], n), (Q[:, 2 * n:3 * n], T.IDb[:], Y[:, lo:hi], n)], yk + zk + ["IDb"], ["B6.v"])
+        V(n, lambda v: v.tensor_tensor_scan(b("ps")[:], T.rs[:, 0:n], Q[:, n:2 * n], 0.0, A.min, A.max), ["B6.y", "rs"], [K("ps")])
+        V(n, lambda v: v.tensor_scalar(b("v")[:], Q[:, 2 * n:3 * n], 0.5, -0.25, A.mult, A.add), ["B6.v"], [K("v")])
+        pl = lambda k: b("pl")[:, 12 * k:12 * k + m]
+        V(m, lambda v: v.tensor_scalar(pl(0), b("ps")[:, 15:n:16], 15, None, A.bitwise_and), [K("ps")], [K("p0")])
+        V(m, lambda v: v.tensor_tensor(pl(1), pl(0), T.iB[:, 3 * p:3 * p + m], A.add), [K("p0"), "iB"], [K("p1")])
+        V(m, lambda v: v.tensor_scalar(b("Po")[:, 0:m], pl(1), col(7), None, A.add), [K("p1"), "c7"], [K("Po")])
+
+        step(t, "rows%d" % c)
+
+        def write():
+            step(t, "write")
+            op("V", 0.05 + n * 3.8 * CY, lambda: g.vector.tensor_copy(Xn[:, :].indirect(b("Po")[:, 0:m]), b("v")[:]), [K("v"), K("Po"), "xcopy"], keys("X%d" % xat[t + 1], c if DUAL[t] else 0, 1 if DUAL[t] else 2))
+        V(n, lambda v: v.tensor_tensor(b("rd")[:], D[:, n:2 * n], hm[:, n:2 * n], A.add), [bk + ".S", K("hm")], [K("rd")])
+        V(n, lambda v: v.tensor_tensor(b("fl")[:], b("rd")[:], D[:, n:2 * n], A.is_lt), [bk + ".S", K("rd")], [K("fl")])
+        V(n, lambda v: v.tensor_tensor(U[:, 0:n], U[:, 0:n], b("fl")[:], A.mult), ["B5.d", K("fl")], ["B5.d"])
+        V(n, lambda v: v.tensor_tensor(b("R")[:], Sh, U[:, 0:n], A.add), ["B5.d"] + kS, [K("R")])
         if not last:
-            V(n, lambda v: v.tensor_tensor(T.B6[:, n:2 * n], T.B6[:, n:2 * n], c3, A.mult), ["B6.e", "C3_%d_%d" % (t, c)], ["B6.e"])
-            V(n, lambda v: v.tensor_tensor(En[:, n:2 * n], E[:, n:2 * n], T.B6[:, n:2 * n], A.add), ["B6.e", ke], [K("e%d" % nxt)])
-            V(n, lambda v: v.tensor_scalar(b("Eo")[:], En[:, n:2 * n], float(OFS), None, A.add), [K("e%d" % nxt)], [K("Eo")], 0.5)
-            V(n, lambda v: v.tensor_tensor(b("bd")[:], b("bd")[:], T.B4[:, 0:n], A.add), ["B4.h", K("bd")], [K("bd")])
-        P([(T.B6[:, 2 * n:3 * n], T.ShI[:], b("R")[:], n), (T.B6[:, 2 * n:3 * n], T.E00h[:], Wm[:, 0:n], n), (T.B6[:, 2 * n:3 * n], T.E0h[:], Wm[:, n:2 * n], n),
-           (T.B6[:, 2 * n:3 * n], T.E0h[:], Wm[:, 2 * n:3 * n], n)], [K("R"), K("Wm"), "ShI", "E00h", "E0h"], ["B6.s"])
-        P([(T.B6[:, 3 * n:4 * n], T.IDb[:], Y[:, lo:hi], n), (T.B6[:, 3 * n:4 * n], T.IDb[:], Z[:, lo:hi], n)], yk + zk + ["IDb"], ["B6.y"])
-        V(n, lambda v: v.tensor_scalar(b("v")[:], T.B6[:, 3 * n:4 * n], 0.5, -0.25, A.mult, A.add), ["B6.y"], [K("v")])
-        op("V", 0.05 + n * 3 * CY, lambda: g.vector.tensor_copy(Xn[:, :].indirect(b("Po")[:, 0:m]), b("v")[:]), [K("v"), K("Po"), "X.%d.all" % nxt], ["X.%d.%d" % (nxt, c)])
-        V(n, lambda v: v.tensor_tensor(T.B6[:, 2 * n:3 * n], T.B6[:, 2 * n:3 * n], hm[:, n:2 * n], A.mult), ["B6.s", K("hm")], ["B6.s"])
-        V(n, lambda v: v.tensor_tensor(En[:, 2 * n:3 * n], b("R")[:], T.B6[:, 2 * n:3 * n], A.add), ["B6.s", K("R")], [K("S%d" % nxt)])
-        if not last:
-            V(n, lambda v: v.tensor_scalar(b("So")[:], En[:, 2 * n:3 * n], float(OFS), None, A.add), [K("S%d" % nxt)], [K("So")], 0.5)
-        else:
-            V(n, lambda v: v.tensor_scalar(T.yso[:, lo:hi], En[:, 2 * n:3 * n], float(OFS), None, A.add), [K("S%d" % nxt)], ["yso%d" % c])
+            V(n, lambda v: v.tensor_tensor(U[:, n:2 * n], U[:, n:2 * n], c3, A.mult), ["B5.e", "C3_%d_%d" % (t, c)], ["B5.e"])
+            for u, k, d in moves(t, c):
+                V(k * B, lambda v, u=u, k=k, d=d: v.tensor_tensor(cut(T.eh, d, k), cut(T.eh, p + u // B, k), U[:, n + u:n + u + k * B], A.add), ["B5.e"] + keys("eh", p + u // B, k), keys("eh", d, k))
+                cs(cut(T.Eo, d, k), cut(T.eh, d, k), k * B // 2, float(OFS), A.add, keys("eh", d, k), keys("Eo", d, k))
+        P([(U[:, 2 * n:3 * n], T.E00h[:], Wm[:, 0:n], n), (U[:, 2 * n:3 * n], T.E0h[:], Wm[:, n:2 * n], n), (U[:, 2 * n:3 * n], T.E0h[:], Wm[:, 2 * n:3 * n], n),
+           (U[:, 2 * n:3 * n], T.ShI[:], b("R")[:], n)], [K("R"), "ShI", "E00h", "E0h"] + wk, ["B5.s"])
+        V(n, lambda v: v.tensor_tensor(U[:, 2 * n:3 * n], U[:, 2 * n:3 * n], hm[:, 0:n], A.mult), ["B5.s", K("hm")], ["B5.s"])
+        for u, k, d in moves(t, c):
+            V(k * B, lambda v, u=u, k=k, d=d: v.tensor_tensor(cut(T.Sh, d, k), b("R")[:, u:u + k * B], U[:, 2 * n + u:2 * n + u + k * B], A.add), ["B5.s", K("R")], keys("Sh", d, k))
+            if not last:
+                cs(cut(T.So, d, k), cut(T.Sh, d, k), k * B // 2, float(OFS), A.add, keys("Sh", d, k), keys("So", d, k))
+            else:
+                cs(T.yso[:, lo:hi], Sh, n, float(OFS), A.add, kS, ["yso%d" % c])
+        return write
 
     def copyX(t):
-        par, nxt = t % 2, (t + 1) % 2
-        op("Y", 0.1, lambda: g.sync.dma_start(T["X%d" % nxt][:], T["X%d" % par][:]), ["X.%d.%d" % (par, k) for k in range(NC)],
-           ["X.%d.%d" % (nxt, k) for k in range(NC)] + ["X.%d.all" % nxt], sem="xc%d" % t, x=4.5)
+        op("Y", 0.1, lambda: g.sync.dma_start(T["X%d" % xat[t + 1]][:], T["X%d" % xat[t]][:]), keys("X%d" % xat[t], 0, 2), keys("X%d" % xat[t + 1], 0, 2) + ["xcopy"], sem="xc%d" % t, x=5.0)
 
     def plans(t0, t1):
         w = 12 * (t1 - t0)
+        step(t1, "plans")
         P([(T.B7[:, 0:w], win("WD16", k), T.C3[:, t0 * I + k:t1 * I:16], w) for k in range(16)], ["WD16"] + ["C3_%d_%d" % (t, c) for t in range(t0, t1) for c in range(NC)], ["B7.f"])
         for t in range(t0, t1):
             q = T.B7[:, 12 * (t - t0):12 * (t - t0 + 1)]
             ph = T.phl[:, 12 * t:12 * t + 12]
-            V(12, lambda v, ph=ph: v.tensor_tensor(T.Pt[:], ph, T.Pl[:], A.subtract), ["Pl", "ph%d" % t], ["Pt"])
+            p = 3 * at(t, 0)
+            Pl, Al = T.Pl[:, p:p + 12], T.Al[:, p:p + 12]
+            V(12, lambda v, ph=ph, Pl=Pl: v.tensor_tensor(T.Pt[:], ph, Pl, A.subtract), ["Pl"] + keys("ph%d" % t, 0, 2), ["Pt"])
             V(12, lambda v, q=q: v.tensor_tensor(T.Pt2[:], T.Pt[:], q, A.mult), ["Pt", "B7.f"], ["Pt2"])
-            V(12, lambda v: v.tensor_tensor(T.Pl[:], T.Pl[:], T.Pt2[:], A.add), ["Pt2", "Pl"], ["Pl"])
+            V(12, lambda v, Pl=Pl: v.tensor_tensor(Pl, Pl, T.Pt2[:], A.add), ["Pt2", "Pl"], ["Pl"])
             if t == 0:
-                V(12, lambda v, q=q: v.tensor_copy(T.Al[:], q), ["B7.f"], ["Al"])
+                V(12, lambda v, q=q, Al=Al: v.tensor_copy(Al, q), ["B7.f"], ["Al"])
             else:
-                V(12, lambda v, q=q: v.tensor_tensor(T.Al[:], T.Al[:], q, A.add), ["B7.f", "Al"], ["Al"])
+                V(12, lambda v, q=q, Al=Al: v.tensor_tensor(Al, Al, q, A.add), ["B7.f", "Al"], ["Al"])
+            if t < RO - 1:
+                for nm in ("Pl", "Al"):
+                    V(3, lambda v, nm=nm, p=p: v.tensor_copy(T[nm][:, p - 3:p], T[nm][:, p + 9:p + 12]), [nm], [nm])
 
+    def ahead(t, c):
+        zprep(t, c)
+        if HC:
+            zhash(t, c, c + 1)
+        elif c == 1:
+            zhash(t, 0, 2)
     for c in range(NC):
-        zprep(0, c)
-    zhash(0)
+        ahead(0, c)
+    for k in range(16):
+        S(128, lambda s, k=k: s.activation(T.WI[:, 128 * k:128 * k + 128], T.IDb[:], F.Copy, scale=float(k + 1)), ["IDb"], ["WI%d" % k])
     for t in range(RO):
         for c in range(NC):
             bulk(t, c)
-        copyX(t)
+        if DUAL[t]:
+            copyX(t)
+        if t in (3, RO - 1):
+            plans(0 if t == 3 else 3, t)
         if t == RO - 1:
-            plans(0, t)
-            for k in range(16):
-                cs(T.WI[:, 128 * k:128 * k + 128], T.IDb[:], 64, float(k + 1), A.mult, ["IDb"], ["WI%d" % k])
-            for c, (lo, hi) in enumerate(CH):
-                V(hi - lo, lambda v, c=c, lo=lo, hi=hi: v.tensor_scalar(T.yfo[:, lo:hi], T["fb_%d" % c][:], -1024.0, None, A.add), ["fb_%d" % c], ["yfo%d" % c], 0.5)
-            op("Y", 0.1, lambda: g.sync.dma_start(T.yf[:], T.yfo[:]), ["yfo%d" % c for c in range(NC)], ["yf"], sem="o0", x=2.0)
+            cs(T.yfo[:], T.fb[:, 0:I], I // 2, -1024.0, A.add, keys("fb", 0, 4), ["yfo"])
+            op("Y", 0.1, lambda: g.sync.dma_start(T.yf[:], T.yfo[:]), ["yfo"], ["yf"], sem="o0", x=2.0)
+        writes = []
         for c in range(NC):
             reduce(t, c)
-            control(t, c)
-            if t < RO - 1:
-                zprep(t + 1, c)
+            writes.append(control(t, c))
+            if DUAL[t]:
+                writes.pop()()
+        for w in writes:
+            w()
         if t < RO - 1:
-            zhash(t + 1)
+            for c in range(NC):
+                ahead(t + 1, c)
     plans(RO - 1, RO)
-    V(12, lambda v: v.tensor_scalar(T.Pt[:], T.Al[:], 1024.0, None, A.mult), ["Al"], ["Pt"])
-    V(12, lambda v: v.tensor_tensor(T.ypo[:], T.Pl[:], T.Pt[:], A.add), ["Pl", "Pt"], ["ypo"])
+    V(12, lambda v: v.tensor_scalar(T.Pt[:], T.Al[:, 0:12], 1024.0, None, A.mult), ["Al"], ["Pt"])
+    V(12, lambda v: v.tensor_tensor(T.ypo[:], T.Pl[:, 0:12], T.Pt[:], A.add), ["Pl", "Pt"], ["ypo"])
     op("Y", 0.1, lambda: g.sync.dma_start(T.yp[:], T.ypo[:]), ["ypo"], ["yp"], sem="o1", x=2.0)
-    op("Y", 0.1, lambda: g.sync.dma_start(T.ys[:], T.yso[:]), ["yso%d" % c for c in range(NC)], ["ys"], sem="o2", x=2.0)
-    XF = T["X%d" % (RO % 2)]
-    for c, (lo, hi) in enumerate(CH):
-        bk = "B%d" % (c % 2)
-        P([(T[bk][:, 0:hi - lo], T.WI[:, 128 * k:128 * k + 128], XF[:, 16 * lo + k:16 * hi:16], hi - lo) for k in range(16)],
-          ["WI%d" % k for k in range(16)] + ["X.%d.%d" % (RO % 2, c)], [bk + ".P"])
-        V(hi - lo, lambda v, bk=bk, lo=lo, hi=hi: v.tensor_copy(T.yxo[:, lo:hi], T[bk][:, 0:hi - lo]), [bk + ".P"], ["yxo%d" % c])
+    op("Y", 0.1, lambda: g.sync.dma_start(T.ys[:], T.yso[:]), ["yso0", "yso1"], ["ys"], sem="o2", x=2.0)
+    XF = T["X%d" % xat[RO]]
+    for c in range(NC):
+        bk = "B%d" % (2 + c)
+        lo, hi = c * n, c * n + n
+        P([(T[bk][:, 0:n], T.WI[:, 128 * k:128 * k + 128], XF[:, 16 * lo + k:16 * hi:16], n) for k in range(16)],
+          ["WI%d" % k for k in range(16)] + keys("X%d" % xat[RO], c), [bk + ".d"])
+        S(n, lambda s, bk=bk, lo=lo, hi=hi: s.activation(T.yxo[:, lo:hi], T[bk][:, 0:n], F.Copy), [bk + ".d"], ["yxo%d" % c])
         op("Y", 0.1, lambda lo=lo, hi=hi: g.sync.dma_start(T.yx[:, lo:hi], T.yxo[:, lo:hi]), ["yxo%d" % c], ["yx%d" % c], sem="o%d" % (3 + c), x=2.0)
 
-    engs = ["V", "S", "P", "G", "Y", "N"]
-    order, when = schedule(ops, engs)
+    if not ORDER:
+        ORDER.extend(schedule(ops, ["V", "S", "P", "G", "Y", "N"]))
     count = {}
     done = {}
     seen = {}
-    for i in order:
+    for i in ORDER:
         o = ops[i]
         e = o["e"]
         if e != "N":
             for d, raw in sorted(o["dep"].items()):
                 od = ops[d]
-                if od["e"] == e and not raw and od["sem"] is None:
+                if od["e"] == e == "P" and not raw:
                     continue
                 if d not in done:
                     continue

from concourse.bass import DstId, RemoteDMATransfer
from concourse.mybir import AluOpType as A, ActivationFunctionType as F

N, I, W, PLN, RO, B = 4, 192, 3072, 1024, 6, 48
NC, n, m = 2, 96, 6
ZM = [1, 1, 1, 1]
ZQ = [(0, 1, "VVVVVVVVVVVVGGGG"), (1, 2, "GGGGGGGGVVVVVVVV"), (2, 4, "VVVVVVVVGGGGSSSS")]
TO = ["SP", "SP"]
PG = 4
HC = True
DUAL = [0, 0, 0, 0, 0, 1]
PEC = 0.00044
VF = 1.05
LAT = 0.2
NET = 5.0
SLACK = 0.05
PASSES = 4
STEPS = {"bulk0": 5, "top0": 10, "bulk1": 20, "top1": 30, "write": 40, "rows0": 50, "rows1": 55, "z0": -38, "z1": -40, "z2": 15, "z3": 15, "f0": 8, "f1": 22, "plans": 60}
OFS = 1536
EPS = 3.0 / 128
BO = 2040
BIG = 262144.0
RB = RO + 3

SCRATCH = {
    "pli": ("sbuf", [128, PLN], "int32"), "s0i": ("sbuf", [128, I], "int32"), "thi": ("sbuf", [128, I], "int32"),
    "p0i": ("sbuf", [128, 12], "int32"), "f0b": ("sbuf", [128, I], "bfloat16"),
    "X0": ("sbuf", [128, W], "bfloat16"), "X1": ("sbuf", [128, W], "bfloat16"),
    "pid": ("sbuf", [128, 1], "int32"), "pmi": ("sbuf", [128, 1], "int32"), "cols": ("sbuf", [128, 16], "float32"),
    "iC": ("sbuf", [128, 144], "float32"), "iG": ("sbuf", [128, 128], "float32"), "iM": ("sbuf", [128, I], "float32"),
    "iB": ("sbuf", [128, 36], "int32"), "h": ("sbuf", [128, 96], "int32"), "hf": ("sbuf", [128, 12], "float32"), "hs": ("sbuf", [128, I], "int32"),
    "Ho": ("sbuf", [128, 12], "uint16"), "P0u": ("sbuf", [128, 12], "uint16"),
    "WI": ("sbuf", [128, 16 * 128], "bfloat16"), "C3": ("sbuf", [128, RO * I], "bfloat16"), "phl": ("sbuf", [128, RO * 12], "int32"),
    "Pl": ("sbuf", [128, 3 * RB], "float32"), "Pt": ("sbuf", [128, 12], "float32"), "Pt2": ("sbuf", [128, 12], "float32"),
    "Al": ("sbuf", [128, 3 * RB], "float32"), "ypo": ("sbuf", [128, 12], "float32"),
    "yso": ("sbuf", [128, I], "float32"), "yfo": ("sbuf", [128, I], "bfloat16"), "yxo": ("sbuf", [128, I], "float32"),
    "mk": ("sbuf", [128, I], "bfloat16"), "rs": ("sbuf", [128, I], "bfloat16"), "rs1": ("sbuf", [128, I], "bfloat16"),
    "EH0": ("sbuf", [128, I], "float16"), "EH1": ("sbuf", [128, I], "float16"),
}
for _k in ("BD", "IDb", "nIDb", "LS", "LI", "WUB", "tmpc", "tmpe"):
    SCRATCH[_k] = ("sbuf", [128, 128], "bfloat16")
for _k in ("WD", "WDn", "WD2", "WD16"):
    SCRATCH[_k] = ("sbuf", [128, 144], "bfloat16")
for _k in ("BDh", "R0h", "E00h", "E0h", "IDh", "nIDh", "ID64", "ShI"):
    SCRATCH[_k] = ("sbuf", [128, 128], "float16")
for _k, _dt in (("Sh", "float16"), ("eh", "float16"), ("bd", "float16"), ("fb", "float16"), ("So", "uint16"), ("Eo", "uint16")):
    SCRATCH[_k] = ("sbuf", [128, RB * B], _dt)
for _k in ("ZR", "dS", "dP", "gS", "aP"):
    SCRATCH[_k] = ("sbuf", [128, W], "bfloat16")
for _t in range(RO):
    SCRATCH["Z%d" % _t] = ("sbuf", [128, I], "bfloat16")
    SCRATCH["Y%d" % _t] = ("sbuf", [128, I], "bfloat16")
for _c in range(NC):
    for _nm, _sh, _dt in (("rl", 2 * n, "bfloat16"), ("hm", 2 * n, "bfloat16"), ("Wm", 3 * n, "float16"), ("fl", n, "float16"), ("rd", n, "int32"),
                          ("R", n, "float16"), ("ts", n, "float32"), ("y0", n, "float32"), ("v", n, "int32"),
                          ("ps", n, "int32"), ("pl", 32, "int32"), ("To", 12, "uint16"), ("Po", 12, "uint16")):
        SCRATCH["%s_%d" % (_nm, _c)] = ("sbuf", [128, _sh], _dt)
for _k in range(8):
    SCRATCH["B%d" % _k] = ("psum", [128, 512], "float32")

LOADS = ["x0", "s0", "z0", "z1", "pl", "p0", "f0", "th"]
SEMAPHORES = ["V", "S", "P", "G", "sent"] + ["ld_" + k for k in LOADS] + ["xc%d" % t for t in range(RO)] + ["o%d" % k for k in range(8)]
SEMAPHORES += ["a%d_%d" % (t, j) for t in range(RO - 1) for j in range(3)]

CY = 0.00083 * VF
ORDER = []


def schedule(ops, eng_list):
    cnt = len(ops)
    succ = [[] for _ in range(cnt)]
    for i, o in enumerate(ops):
        for d in o["dep"]:
            succ[d].append(i)
    pred = [list(o["dep"]) for o in ops]
    gap = lambda i, j: 0.0 if ops[i]["e"] == ops[j]["e"] == "P" else LAT

    def run(before, after, prio, back):
        left = [len(x) for x in before]
        ready, free = {}, {}
        for e in eng_list:
            ready[e], free[e] = [], 0.0
        est, end = [0.0] * cnt, [0.0] * cnt
        for i in range(cnt):
            if not left[i]:
                est[i] = ops[i]["x"] if back else 0.0
                ready[ops[i]["e"]].append(i)
        order = []
        while len(order) < cnt:
            best = None
            for e in eng_list:
                if not ready[e]:
                    continue
                f = free[e]
                lowest = max(f, min(est[i] for i in ready[e])) + SLACK
                j = max((i for i in ready[e] if est[i] <= lowest), key=lambda i: prio[i])
                k = (max(f, est[j]), -prio[j], j)
                if best is None or k < best:
                    best = k
            st, _, j = best
            o = ops[j]
            ready[o["e"]].remove(j)
            order.append(j)
            if o["e"] != "N":
                free[o["e"]] = st + o["c"]
            end[j] = st + o["c"] + (0.0 if back else o["x"])
            for s in after[j]:
                left[s] -= 1
                x = end[j] + gap(s, j) + (ops[s]["x"] if back else 0.0)
                if x > est[s]:
                    est[s] = x
                if not left[s]:
                    ready[ops[s]["e"]].append(s)
        return order, end
    prio = [0.0] * cnt
    for i in range(cnt - 1, -1, -1):
        prio[i] = max([prio[s] for s in succ[i]] + [-ops[i]["ph"] - i / cnt])
    best = None
    for _ in range(PASSES):
        order, end = run(pred, succ, prio, False)
        if best is None or max(end) < best[0]:
            best = (max(end), order)
        prio = run(succ, pred, end, True)[1]
    return best[1]


def rank_program(g, core, T, topo):
    rank = T.rank_of(core)
    if rank is None:
        return
    ops = []
    last_w, last_r = {}, {}
    banks = {}
    phase = [0]

    def step(t, name):
        phase[0] = 100 * t + STEPS[name]
    queue = {"V": g.vector, "S": g.scalar, "P": g.tensor, "G": g, "Y": g.sync, "N": None}

    def op(e, c, fn, r=(), w=(), sem=None, x=0.0, inc=None):
        i = len(ops)
        dep = {}

        def need(j, raw):
            if j != i:
                dep[j] = dep.get(j, False) or raw
        for k in r:
            if k in last_w:
                need(last_w[k], True)
        for k in w:
            if k in last_w:
                need(last_w[k], False)
            for j in last_r.get(k, ()):
                need(j, False)
        bs = set(k[:2] for k in tuple(r) + tuple(w) if k[0] == "B" and k[2:3] == ".")
        for b in bs:
            cur = banks.setdefault(b, [e, [], []])
            if cur[0] != e:
                cur[0], cur[1], cur[2] = e, cur[2], []
            for j in cur[1]:
                need(j, False)
            cur[2].append(i)
        for k in r:
            last_r.setdefault(k, []).append(i)
        for k in w:
            last_w[k] = i
            last_r[k] = []
        ops.append({"e": e, "c": c, "x": x, "fn": fn, "dep": dep, "sem": sem, "inc": inc, "ph": phase[0]})
        return i

    def V(w_, fn, r, w, f=1.0):
        op("V", max(64, w_ * f) * CY, lambda: fn(g.vector), r, w)

    def VG(w_, fn, r, w):
        op("V", 0.05 + w_ * 1.56 * CY, lambda: fn(g.vector), r, w)

    def S(w_, fn, r, w):
        op("S", 0.06 + w_ * CY, lambda: fn(g.scalar), r, w)

    def copy(e, w_, out, src, r, w):
        if e == "V":
            V(w_, lambda v: v.tensor_copy(out, src), r, w, 0.5)
        elif e == "S":
            S(w_, lambda s: s.activation(out, src, F.Copy), r, w)
        else:
            op("G", 0.19 + 2 * w_ * CY, lambda: g.affine_select(out, src, [[0, w_]], A.is_ge, 0.0, 0, 0), r, w)

    def P(mms, r, w, first=True, last=True):
        def fn():
            k = len(mms)
            for j, (o, l, rr, _) in enumerate(mms):
                ins = g.tensor.matmul(o, l, rr, first and j == 0, last and j == k - 1)
            return ins
        op("P", sum(max(64, x[3]) for x in mms) * PEC, fn, r, w)

    at = lambda t, j: RO - 1 - t + j
    cut = lambda buf, p, k=1: buf[:, p * B:(p + k) * B]
    keys = lambda nm, p, k=1: ["%s.%d" % (nm, q) for q in range(p, p + k)]

    def moves(t, c):
        if c == 0 or t == RO - 1:
            return [(0, 2, at(t, 2 * c))]
        return [(0, 1, at(t, 2)), (B, 1, at(t + 1, 0))]

    def load(e, name, dst, src, w, x):
        op(e, 0.1, lambda: queue[e].dma_start(dst, src), (), w, sem="ld_" + name, x=x)
    load("Y", "x0", T.X0[:], T.x0[:], ["X0.0", "X0.1"], 5.0)
    load("S", "z0", T.Z0[:, 0:3 * B], T.z0[:, B:I], keys("Z0", 0, 3), 2.2)
    load("S", "s0", T.s0i[:], T.s0[:], ["s0i"], 2.5)
    load("S", "p0", T.p0i[:], T.p0[:], ["p0i"], 2.0)
    load("Y", "pl", T.pli[:], T.pl[:], ["pli"], 5.0)
    load("S", "z1", T.Z0[:, 3 * B:I], T.z0[:, 0:B], keys("Z0", 3), 2.2)
    load("S", "th", T.thi[:], T.th[:], ["thi"], 2.5)
    load("S", "f0", T.f0b[:], T.f0[:], ["f0b"], 2.2)

    op("G", 0.15, lambda: g.iota(T.pid[:], [[1, 1]], 0, 1), (), ["pid"])
    op("G", 0.4, lambda: g.iota(T.iC[:], [[1, 144]], 0, 0, allow_small_or_imprecise_dtypes=True), (), ["iC"])
    op("G", 0.4, lambda: g.iota(T.iG[:], [[16, 8], [0, 16]], 0, 0, allow_small_or_imprecise_dtypes=True), (), ["iG"])
    op("G", 0.5, lambda: g.iota(T.iM[:], [[0, 12], [1, 16]], 0, 0, allow_small_or_imprecise_dtypes=True), (), ["iM"])
    op("G", 0.2, lambda: g.iota(T.iB[:], [[0, 3], [256, 12]], 0, 0), (), ["iB"])
    col = lambda k: T.cols[:, k:k + 1]
    V(1, lambda v: v.tensor_scalar(T.pmi[:], T.pid[:], 15, None, A.bitwise_and), ["pid"], ["pmi"])
    V(1, lambda v: v.tensor_copy(col(0), T.pid[:]), ["pid"], ["c0"])
    V(1, lambda v: v.tensor_copy(col(1), T.pmi[:]), ["pmi"], ["c1"])
    V(1, lambda v: v.tensor_tensor(col(2), col(0), col(1), A.subtract), ["c0", "c1"], ["c2"])
    V(1, lambda v: v.tensor_scalar(col(3), col(2), 15.0, None, A.add), ["c2"], ["c3"])
    V(1, lambda v: v.tensor_scalar(col(4), col(0), 1.0, None, A.add), ["c0"], ["c4"])
    V(1, lambda v: v.tensor_scalar(col(5), col(1), 0.0, None, A.is_equal), ["c1"], ["c5"])
    V(1, lambda v: v.tensor_scalar(col(6), col(1), 2.0, 1.0, A.mult, A.add), ["c1"], ["c6"])
    V(1, lambda v: v.tensor_scalar(col(7), col(1), 16.0, None, A.mult), ["c1"], ["c7"])

    def cs(out, src, w_, c, o0, r, w, c2=None, o1=None):
        if o1 is None:
            V(w_, lambda v: v.tensor_scalar(out, src, c, None, o0), r, w)
        else:
            V(w_, lambda v: v.tensor_scalar(out, src, c, c2, o0, o1), r, w)

    def sc(out, src, w_, c, r, w):
        cs(out, src, w_ // 2, c, A.mult, r, w)
    cs(T.WD[:], T.iC[:], 144, col(3), A.is_equal, ["iC", "c3"], ["WD"])
    sc(T.WDn[:], T.WD[:], 144, -1.0, ["WD"], ["WDn"])
    sc(T.WD2[:], T.WD[:], 144, -2.0, ["WD"], ["WD2"])
    sc(T.WD16[:], T.WD[:], 144, 1.0 / 16, ["WD"], ["WD16"])
    cs(T.BD[:], T.iG[:], 128, col(2), A.is_equal, ["iG", "c2"], ["BD"])
    sc(T.WUB[:], T.BD[:], 128, col(6), ["BD", "c6"], ["WU"])
    cs(T.IDb[:], T.iC[:, 0:128], 128, col(0), A.is_equal, ["iC", "c0"], ["IDb"])
    cs(T.mk[:], T.iM[:], 192, col(1), A.not_equal, ["iM", "c1"], ["mk"], -BIG / 2, A.mult)
    S(192, lambda s: s.activation(T.rs1[:], T.iM[:], F.Sigmoid, bias=-512.0, scale=1024.0), ["iM"], ["rs1"])
    cs(T.rs[:], T.rs1[:], 96, 2 * BIG, A.mult, ["rs1"], ["rs"], -BIG, A.add)
    cs(T.tmpc[:], T.iC[:, 0:128], 128, col(0), A.is_gt, ["iC", "c0"], ["tmpc"])
    V(256, lambda v: v.tensor_tensor(T.LS[:], T.tmpc[:], T.BD[:], A.mult), ["tmpc", "BD"], ["LS"])
    V(256, lambda v: v.tensor_tensor(T.LI[:], T.LS[:], T.IDb[:], A.subtract), ["LS", "IDb"], ["LI"])
    sc(T.IDh[:], T.IDb[:], 128, 1.0, ["IDb"], ["IDh"])
    if any(ZM):
        sc(T.nIDb[:], T.IDb[:], 128, -1.0, ["IDb"], ["nIDb"])
    sc(T.nIDh[:], T.IDb[:], 128, -1.0, ["IDb"], ["nIDh"])
    sc(T.ID64[:], T.IDb[:], 128, 64.0, ["IDb"], ["ID64"])
    sc(T.BDh[:], T.BD[:], 128, 1.0, ["BD"], ["BDh"])
    sc(T.R0h[:], T.BD[:], 128, col(5), ["BD", "c5"], ["R0h"])
    sc(T.E00h[:], T.IDb[:], 128, col(5), ["IDb", "c5"], ["E00h"])
    sc(T.E0h[:], T.WD[:, 15:143], 128, 1.0, ["WD"], ["E0h"])
    cs(T.tmpe[:], T.iC[:, 0:128], 128, col(4), A.is_equal, ["iC", "c4"], ["tmpe"])
    V(256, lambda v: v.tensor_tensor(T.tmpc[:], T.tmpe[:], T.BD[:], A.mult), ["tmpe", "BD"], ["tmpc"])
    V(256, lambda v: v.tensor_tensor(T.ShI[:], T.tmpc[:], T.IDb[:], A.subtract), ["tmpc", "IDb"], ["ShI"])

    for j, k, b0 in ((0, 3, 1), (3, 1, 0)):
        p, w_ = at(0, j), k * B
        V(12, lambda v, j=j, k=k, b0=b0: v.tensor_copy(T.P0u[:, 3 * j:3 * (j + k)], T.p0i[:, 3 * b0:3 * (b0 + k)]), ["p0i"], ["P0u.%d" % j])
        V(12, lambda v, p=p, k=k, b0=b0: v.tensor_copy(T.Pl[:, 3 * p:3 * (p + k)], T.p0i[:, 3 * b0:3 * (b0 + k)]), ["p0i"], ["Pl"])
        V(w_, lambda v, p=p, k=k, b0=b0: v.tensor_copy(cut(T.So, p, k), cut(T.s0i, b0, k)), ["s0i"], keys("So", p, k))
        cs(cut(T.Sh, p, k), cut(T.s0i, b0, k), w_, -float(OFS), A.add, ["s0i"], keys("Sh", p, k))
        cs(cut(T.fb, p, k), cut(T.f0b, b0, k), w_ // 2, 1024.0, A.add, ["f0b"], keys("fb", p, k))
        cs(cut(T.bd, p, k), cut(T.thi, b0, k), w_, -float(BO), A.add, ["thi"], keys("bd", p, k))
    for c in range(NC):
        p = at(0, 2 * c)
        VG(n, lambda v, c=c, p=p: v.tensor_scalar(cut(T.eh, p, 2), T.pli[:, :].indirect(T.P0u[:, m * c:m * c + m]), -float(OFS), None, A.add), ["pli", "P0u.0", "P0u.3"], keys("eh", p, 2))
        cs(cut(T.Eo, p, 2), cut(T.eh, p, 2), n // 2, float(OFS), A.add, keys("eh", p, 2), keys("Eo", p, 2))

    win = lambda nm, k: T[nm][:, 15 - k:143 - k]
    subs = [0]
    xat = [sum(DUAL[:t]) % 2 for t in range(RO + 1)]

    def zprep(t, c):
        Z, zn = T["Z%d" % t], "Z%d" % t
        for j0, j1, qs in ZQ:
            if j0 // 2 == c:
                step(t, "z%d" % j0)
                for k in range(16):
                    copy(qs[k], (j1 - j0) * B, T.ZR[:, 16 * B * j0 + k:16 * B * j1:16], cut(Z, j0, j1 - j0), keys(zn, j0, j1 - j0), ["ZR.%d.%d" % (j, k) for j in range(j0, j1)])
        p = at(t, 2 * c)
        step(t, "f%d" % c)
        if c == 0 and t:
            old, ok = [(T.B7[:, 0:B], T.IDh[:], cut(T.fb, p + 4), B), (T.B7[:, B:n], T.IDh[:], cut(T.fb, p + 1), B)], keys("fb", p + 4) + keys("fb", p + 1)
        else:
            old, ok = [(T.B7[:, 0:n], T.IDh[:], cut(T.fb, p, 2), n)], keys("fb", p, 2)
        P([(T.B7[:, 0:n], T.IDb[:], cut(Z, 2 * c, 2), n)] + old, ok + ["IDh", "IDb"] + keys(zn, 2 * c, 2), ["B7.f"])
        V(n, lambda v: v.tensor_scalar(cut(T.fb, p, 2), T.B7[:, 0:n], 0.5, 511.75, A.mult, A.add), ["B7.f"], keys("fb", p, 2))

    def zhash(t, c0, c1):
        Z = T["Z%d" % t]
        lo, hi = c0 * n, c1 * n
        h = lambda k: T.h[:, 12 * k + m * c0:12 * k + m * c1]
        H = lambda k: "h.%d.%d" % (k, c0)
        ph, hf = T.phl[:, 12 * t + m * c0:12 * t + m * c1], T.hf[:, m * c0:m * c1]
        u = T.B7[:, 256 + lo:256 + hi]
        P([(u, T.IDb[:], T.mk[:, lo:hi], hi - lo), (u, T.WUB[:], Z[:, lo:hi], hi - lo)], ["WU", "mk", "IDb"] + keys("Z%d" % t, 2 * c0, 2 * (c1 - c0)), ["B7.u"])
        V(hi - lo, lambda v: v.tensor_tensor_scan(T.hs[:, lo:hi], T.rs[:, lo:hi], u, 0.0, A.min, A.max), ["B7.u", "rs"], [H(0)])
        V(m, lambda v: v.tensor_scalar(h(1), T.hs[:, lo + 15:hi:16], 4095, None, A.bitwise_and), [H(0)], [H(1)])
        V(m, lambda v: v.tensor_scalar(hf, h(1), 1184.0, None, A.add), [H(1)], [H(2)])
        V(m, lambda v: v.tensor_tensor(h(3), h(1), hf, A.mult), [H(1), H(2)], [H(3)])
        V(m, lambda v: v.tensor_scalar(ph, h(3), 5, 1023, A.logical_shift_right, A.bitwise_and), [H(3)], keys("ph%d" % t, c0, c1 - c0))
        V(m, lambda v: v.tensor_copy(T.Ho[:, m * c0:m * c1], ph), keys("ph%d" % t, c0, c1 - c0), keys("Ho", c0, c1 - c0))
        VG(hi - lo, lambda v: v.tensor_scalar(T["EH%d" % (t % 2)][:, lo:hi], T.pli[:, :].indirect(T.Ho[:, m * c0:m * c1]), -float(OFS), 1.0 / 64, A.add, A.mult),
           ["pli"] + keys("Ho", c0, c1 - c0), keys("EH%d" % (t % 2), c0, c1 - c0))

    def bulk(t, c):
        step(t, "bulk%d" % c)
        X = T["X%d" % xat[t]]
        xk = keys("X%d" % xat[t], 0, 2)
        for j in (2 * c, 2 * c + 1):
            sl = slice(16 * B * j, 16 * B * (j + 1))
            zr = ["ZR.%d.%d" % (j, k) for k in range(16)]
            p = at(t, j)
            VG(16 * B, lambda v, sl=sl, p=p: v.tensor_tensor(T.dS[:, sl], X[:, :].indirect(cut(T.So, p)), T.ZR[:, sl], A.subtract), xk + keys("So", p) + zr, keys("dS", j))
            V(16 * B, lambda v, sl=sl: v.tensor_scalar(T.gS[:, sl], T.dS[:, sl], EPS, None, A.max), keys("dS", j), keys("gS", j), 0.5)
            if not ZM[j]:
                VG(16 * B, lambda v, sl=sl, p=p: v.tensor_tensor(T.dP[:, sl], X[:, :].indirect(cut(T.Eo, p)), T.ZR[:, sl], A.subtract), xk + keys("Eo", p) + zr, keys("dP", j))
                S(16 * B, lambda s, sl=sl: s.activation(T.aP[:, sl], T.dP[:, sl], F.Abs), keys("dP", j), keys("aP", 2 * j, 2))
                continue
            op("S", 0.065 + 16 * B * 1.56 * CY, lambda sl=sl, p=p: g.scalar.activation(T.dP[:, sl], X[:, :].indirect(cut(T.Eo, p)), F.Copy), xk + keys("Eo", p), keys("dP", j))
            for q in range(2):
                bn = "B%d" % (2 + subs[0] % 2)
                subs[0] += 1
                sl = slice(8 * B * (2 * j + q), 8 * B * (2 * j + q + 1))
                P([(T[bn][:, 0:8 * B], T.nIDb[:], T.ZR[:, sl], 8 * B), (T[bn][:, 0:8 * B], T.IDb[:], T.dP[:, sl], 8 * B)], ["IDb", "nIDb"] + keys("dP", j) + zr, [bn + ".d"])
                S(8 * B, lambda s, sl=sl, bn=bn: s.activation(T.aP[:, sl], T[bn][:, 0:8 * B], F.Abs), [bn + ".d"], keys("aP", 2 * j + q))

    def reduce(t, c):
        step(t, "bulk%d" % c)
        bk = "B%d" % c
        D = T[bk]
        p = at(t, 2 * c)
        groups = {"S": (D[:, n:2 * n], [("WD", "dS", keys("dS", 2 * c, 2)), ("WD2", "gS", keys("gS", 2 * c, 2))]), "P": (D[:, 0:n], [("WDn", "aP", keys("aP", 4 * c, 4))])}
        for nm in TO[c]:
            out, streams = groups[nm]
            P([(out, T.IDh[:], cut(T.bd, p, 2), n)], ["IDh"] + keys("bd", p, 2), [bk + "." + nm, bk + ".open"], last=False)
            for j, (wn, src, ks) in enumerate(streams):
                for k0 in range(0, 16, PG):
                    P([(out, win(wn, k), T[src][:, 16 * n * c + k:16 * n * (c + 1):16], n) for k in range(k0, k0 + PG)], [wn] + ks, [bk + "." + nm, bk + ".open"],
                      first=False, last=j == len(streams) - 1 and k0 + PG == 16)

    def control(t, c):
        lo, hi = c * n, c * n + n
        b = lambda nm: T["%s_%d" % (nm, c)]
        K = lambda nm: "%s_%d" % (nm, c)
        p = at(t, 2 * c)
        Sh, e, EH = cut(T.Sh, p, 2), cut(T.eh, p, 2), T["EH%d" % (t % 2)][:, lo:hi]
        kS, ke, kH = keys("Sh", p, 2), keys("eh", p, 2), keys("EH%d" % (t % 2), c)
        X, Xn = T["X%d" % xat[t]], T["X%d" % xat[t + 1]]
        xk = keys("X%d" % xat[t], 0, 2)
        Z, Y = T["Z%d" % t], T["Y%d" % t]
        zk, yk = keys("Z%d" % t, 2 * c, 2), keys("Y%d" % t, 2 * c, 2)
        bk = "B%d" % c
        D = T[bk]
        last = t == RO - 1
        C, U, Q = T.B4, T.B5, T.B6
        step(t, "rows%d" % c)
        P([(U[:, 0:n], T.IDh[:], e, n), (U[:, 0:n], T.nIDh[:], Sh, n)], kS + ke + ["IDh", "nIDh"], ["B5.d"])
        if not last:
            P([(U[:, n:2 * n], T.ID64[:], EH, n), (U[:, n:2 * n], T.nIDh[:], e, n)], kH + ke + ["ID64", "nIDh"], ["B5.e"])
        step(t, "top%d" % c)
        rl = b("rl")
        S(2 * n, lambda s: s.activation(rl[:], D[:, 0:2 * n], F.Sigmoid, bias=(BO - 0.125) * 1024, scale=1024.0), [bk + ".S", bk + ".P"], [K("rl")])
        rP, rS = rl[:, 0:n], rl[:, n:2 * n]
        P([(C[:, n:3 * n], T.LI[:], rl[:], 2 * n), (C[:, n:2 * n], T.BD[:], rS, n)], [K("rl"), "LI", "BD"], ["B4.h"])
        P([(C[:, 0:n], T.BD[:], rS, n), (C[:, 0:n], T.BD[:], rP, n)], [K("rl"), "BD"], ["B4.t"])
        P([(C[:, 3 * n:4 * n], T.LS[:], rS, n)], [K("rl"), "LS"], ["B4.m"])
        P([(C[:, 4 * n:5 * n], T.BD[:], rS, n)], [K("rl"), "BD"], ["B4.c"])
        S(2 * n, lambda s: s.activation(C[:, n:3 * n], C[:, n:3 * n], F.Relu, scale=-1.0), ["B4.h"], ["B4.h"])
        S(n, lambda s: s.activation(C[:, 0:n], C[:, 0:n], F.Relu, bias=64.0, scale=-64.0), ["B4.t"], ["B4.t"])
        Wm = b("Wm")
        for q, (src, ks) in enumerate(((EH, kH + ["B4.t"]), (e, ke + ["B4.h"]), (Sh, kS + ["B4.h"]))):
            V(n, lambda v, q=q, src=src: v.tensor_tensor(Wm[:, q * n:q * n + n], src, C[:, q * n:q * n + n], A.mult), ks, [K("Wm%d" % q)])
        wk = [K("Wm%d" % q) for q in range(3)]
        step(t, "rows%d" % c)
        if not last:
            for u, k, d in moves(t, c):
                V(k * B, lambda v, u=u, k=k, d=d: v.tensor_tensor(cut(T.bd, d, k), cut(T.bd, p + u // B, k), C[:, u:u + k * B], A.add), ["B4.t"] + keys("bd", p + u // B, k), keys("bd", d, k))
        hm = b("hm")
        S(2 * n, lambda s: s.activation(hm[:], C[:, 3 * n:5 * n], F.Relu, bias=1.0, scale=-1.0), ["B4.m", "B4.c"], [K("hm")])
        c3 = T.C3[:, t * I + lo:t * I + hi]
        S(n, lambda s: s.activation(c3, C[:, 0:n], F.Copy, scale=1.0 / 64), ["B4.t"], ["C3_%d_%d" % (t, c)])
        step(t, "top%d" % c)
        P([(Q[:, 0:n], T.IDb[:], T.mk[:, 0:n], n), (Q[:, 0:n], T.R0h[:], Wm[:, 0:n], n), (Q[:, 0:n], T.BDh[:], Wm[:, n:2 * n], n), (Q[:, 0:n], T.BDh[:], Wm[:, 2 * n:3 * n], n)],
          wk + ["R0h", "BDh", "mk", "IDb"], ["B6.t"])
        V(n, lambda v: v.tensor_tensor_scan(b("ts")[:], T.rs[:, 0:n], Q[:, 0:n], 0.0, A.min, A.max), ["B6.t", "rs"], [K("ts")])
        V(m, lambda v: v.tensor_scalar(b("To")[:, 0:m], b("ts")[:, 15:n:16], float(OFS), None, A.add), [K("ts")], [K("To")])
        VG(n, lambda v: v.tensor_tensor(b("y0")[:], X[:, :].indirect(b("To")[:, 0:m]), cut(T.fb, p, 2), A.subtract), xk + [K("To")] + keys("fb", p, 2), [K("y0")])
        S(n, lambda s: s.activation(Y[:, lo:hi], b("y0")[:], F.Abs, bias=1024.0), [K("y0")], yk)
        if not last:
            Zn = T["Z%d" % (t + 1)]
            go = [j for j in (2 * c, 2 * c + 1) if j < 3]
            per = 8 // len(go)

            def send():
                tr = []
                for q, j in enumerate(go):
                    dst = T.cores[(rank + at(t, j) % 4 + t) % N]
                    rid, pc = topo.addr(dst, core)
                    es = topo.engines(core, dst)[q * per:(q + 1) * per]
                    tr.append(RemoteDMATransfer(dst_ids=[DstId(rid=rid, pnc=pc)], dma_engine_mask=sum(1 << x for x in es), remote_sem=T.sem["a%d_%d" % (t, j)],
                                                src=cut(Y, j), dst=cut(Zn, j + 1)))
                g.remote_dma_fused(tr, local_sem=T.sem.sent)
            op("G", 0.7, send, [k for j in go for k in keys("Y%d" % t, j)], [K("net%d" % t)], sem="sent", inc=per * len(go))
            for j in go:
                op("N", 0.0, None, [K("net%d" % t)], keys("Z%d" % (t + 1), j + 1), sem="a%d_%d" % (t, j), inc=per, x=NET)
            if c == 1:
                S(B, lambda s: s.activation(cut(Zn, 0), b("y0")[:, B:n], F.Abs, bias=1024.0), [K("y0")], keys("Z%d" % (t + 1), 0))
        P([(Q[:, n:2 * n], T.IDb[:], T.mk[:, 0:n], n), (Q[:, n:2 * n], T.BD[:], Y[:, lo:hi], n)], yk + ["BD", "mk", "IDb"], ["B6.y"])
        P([(Q[:, 2 * n:3 * n], T.IDb[:], Z[:, lo:hi], n), (Q[:, 2 * n:3 * n], T.IDb[:], Y[:, lo:hi], n)], yk + zk + ["IDb"], ["B6.v"])
        V(n, lambda v: v.tensor_tensor_scan(b("ps")[:], T.rs[:, 0:n], Q[:, n:2 * n], 0.0, A.min, A.max), ["B6.y", "rs"], [K("ps")])
        V(n, lambda v: v.tensor_scalar(b("v")[:], Q[:, 2 * n:3 * n], 0.5, -0.25, A.mult, A.add), ["B6.v"], [K("v")])
        pl = lambda k: b("pl")[:, 12 * k:12 * k + m]
        V(m, lambda v: v.tensor_scalar(pl(0), b("ps")[:, 15:n:16], 15, None, A.bitwise_and), [K("ps")], [K("p0")])
        V(m, lambda v: v.tensor_tensor(pl(1), pl(0), T.iB[:, 3 * p:3 * p + m], A.add), [K("p0"), "iB"], [K("p1")])
        V(m, lambda v: v.tensor_scalar(b("Po")[:, 0:m], pl(1), col(7), None, A.add), [K("p1"), "c7"], [K("Po")])

        step(t, "rows%d" % c)

        def write():
            step(t, "write")
            op("V", 0.05 + n * 3.8 * CY, lambda: g.vector.tensor_copy(Xn[:, :].indirect(b("Po")[:, 0:m]), b("v")[:]), [K("v"), K("Po"), "xcopy"], keys("X%d" % xat[t + 1], c if DUAL[t] else 0, 1 if DUAL[t] else 2))
        V(n, lambda v: v.tensor_tensor(b("rd")[:], D[:, n:2 * n], hm[:, n:2 * n], A.add), [bk + ".S", K("hm")], [K("rd")])
        V(n, lambda v: v.tensor_tensor(b("fl")[:], b("rd")[:], D[:, n:2 * n], A.is_lt), [bk + ".S", K("rd")], [K("fl")])
        V(n, lambda v: v.tensor_tensor(U[:, 0:n], U[:, 0:n], b("fl")[:], A.mult), ["B5.d", K("fl")], ["B5.d"])
        V(n, lambda v: v.tensor_tensor(b("R")[:], Sh, U[:, 0:n], A.add), ["B5.d"] + kS, [K("R")])
        if not last:
            V(n, lambda v: v.tensor_tensor(U[:, n:2 * n], U[:, n:2 * n], c3, A.mult), ["B5.e", "C3_%d_%d" % (t, c)], ["B5.e"])
            for u, k, d in moves(t, c):
                V(k * B, lambda v, u=u, k=k, d=d: v.tensor_tensor(cut(T.eh, d, k), cut(T.eh, p + u // B, k), U[:, n + u:n + u + k * B], A.add), ["B5.e"] + keys("eh", p + u // B, k), keys("eh", d, k))
                cs(cut(T.Eo, d, k), cut(T.eh, d, k), k * B // 2, float(OFS), A.add, keys("eh", d, k), keys("Eo", d, k))
        P([(U[:, 2 * n:3 * n], T.E00h[:], Wm[:, 0:n], n), (U[:, 2 * n:3 * n], T.E0h[:], Wm[:, n:2 * n], n), (U[:, 2 * n:3 * n], T.E0h[:], Wm[:, 2 * n:3 * n], n),
           (U[:, 2 * n:3 * n], T.ShI[:], b("R")[:], n)], [K("R"), "ShI", "E00h", "E0h"] + wk, ["B5.s"])
        V(n, lambda v: v.tensor_tensor(U[:, 2 * n:3 * n], U[:, 2 * n:3 * n], hm[:, 0:n], A.mult), ["B5.s", K("hm")], ["B5.s"])
        for u, k, d in moves(t, c):
            V(k * B, lambda v, u=u, k=k, d=d: v.tensor_tensor(cut(T.Sh, d, k), b("R")[:, u:u + k * B], U[:, 2 * n + u:2 * n + u + k * B], A.add), ["B5.s", K("R")], keys("Sh", d, k))
            if not last:
                cs(cut(T.So, d, k), cut(T.Sh, d, k), k * B // 2, float(OFS), A.add, keys("Sh", d, k), keys("So", d, k))
            else:
                cs(T.yso[:, lo:hi], Sh, n, float(OFS), A.add, kS, ["yso%d" % c])
        return write

    def copyX(t):
        op("Y", 0.1, lambda: g.sync.dma_start(T["X%d" % xat[t + 1]][:], T["X%d" % xat[t]][:]), keys("X%d" % xat[t], 0, 2), keys("X%d" % xat[t + 1], 0, 2) + ["xcopy"], sem="xc%d" % t, x=5.0)

    def plans(t0, t1):
        w = 12 * (t1 - t0)
        step(t1, "plans")
        P([(T.B7[:, 0:w], win("WD16", k), T.C3[:, t0 * I + k:t1 * I:16], w) for k in range(16)], ["WD16"] + ["C3_%d_%d" % (t, c) for t in range(t0, t1) for c in range(NC)], ["B7.f"])
        for t in range(t0, t1):
            q = T.B7[:, 12 * (t - t0):12 * (t - t0 + 1)]
            ph = T.phl[:, 12 * t:12 * t + 12]
            p = 3 * at(t, 0)
            Pl, Al = T.Pl[:, p:p + 12], T.Al[:, p:p + 12]
            V(12, lambda v, ph=ph, Pl=Pl: v.tensor_tensor(T.Pt[:], ph, Pl, A.subtract), ["Pl"] + keys("ph%d" % t, 0, 2), ["Pt"])
            V(12, lambda v, q=q: v.tensor_tensor(T.Pt2[:], T.Pt[:], q, A.mult), ["Pt", "B7.f"], ["Pt2"])
            V(12, lambda v, Pl=Pl: v.tensor_tensor(Pl, Pl, T.Pt2[:], A.add), ["Pt2", "Pl"], ["Pl"])
            if t == 0:
                V(12, lambda v, q=q, Al=Al: v.tensor_copy(Al, q), ["B7.f"], ["Al"])
            else:
                V(12, lambda v, q=q, Al=Al: v.tensor_tensor(Al, Al, q, A.add), ["B7.f", "Al"], ["Al"])
            if t < RO - 1:
                for nm in ("Pl", "Al"):
                    V(3, lambda v, nm=nm, p=p: v.tensor_copy(T[nm][:, p - 3:p], T[nm][:, p + 9:p + 12]), [nm], [nm])

    def ahead(t, c):
        zprep(t, c)
        if HC:
            zhash(t, c, c + 1)
        elif c == 1:
            zhash(t, 0, 2)
    for c in range(NC):
        ahead(0, c)
    for k in range(16):
        S(128, lambda s, k=k: s.activation(T.WI[:, 128 * k:128 * k + 128], T.IDb[:], F.Copy, scale=float(k + 1)), ["IDb"], ["WI%d" % k])
    for t in range(RO):
        for c in range(NC):
            bulk(t, c)
        if DUAL[t]:
            copyX(t)
        if t in (3, RO - 1):
            plans(0 if t == 3 else 3, t)
        if t == RO - 1:
            cs(T.yfo[:], T.fb[:, 0:I], I // 2, -1024.0, A.add, keys("fb", 0, 4), ["yfo"])
            op("Y", 0.1, lambda: g.sync.dma_start(T.yf[:], T.yfo[:]), ["yfo"], ["yf"], sem="o0", x=2.0)
        writes = []
        for c in range(NC):
            reduce(t, c)
            writes.append(control(t, c))
            if DUAL[t]:
                writes.pop()()
        for w in writes:
            w()
        if t < RO - 1:
            for c in range(NC):
                ahead(t + 1, c)
    plans(RO - 1, RO)
    V(12, lambda v: v.tensor_scalar(T.Pt[:], T.Al[:, 0:12], 1024.0, None, A.mult), ["Al"], ["Pt"])
    V(12, lambda v: v.tensor_tensor(T.ypo[:], T.Pl[:, 0:12], T.Pt[:], A.add), ["Pl", "Pt"], ["ypo"])
    op("Y", 0.1, lambda: g.sync.dma_start(T.yp[:], T.ypo[:]), ["ypo"], ["yp"], sem="o1", x=2.0)
    op("Y", 0.1, lambda: g.sync.dma_start(T.ys[:], T.yso[:]), ["yso0", "yso1"], ["ys"], sem="o2", x=2.0)
    XF = T["X%d" % xat[RO]]
    for c in range(NC):
        bk = "B%d" % (2 + c)
        lo, hi = c * n, c * n + n
        P([(T[bk][:, 0:n], T.WI[:, 128 * k:128 * k + 128], XF[:, 16 * lo + k:16 * hi:16], n) for k in range(16)],
          ["WI%d" % k for k in range(16)] + keys("X%d" % xat[RO], c), [bk + ".d"])
        S(n, lambda s, bk=bk, lo=lo, hi=hi: s.activation(T.yxo[:, lo:hi], T[bk][:, 0:n], F.Copy), [bk + ".d"], ["yxo%d" % c])
        op("Y", 0.1, lambda lo=lo, hi=hi: g.sync.dma_start(T.yx[:, lo:hi], T.yxo[:, lo:hi]), ["yxo%d" % c], ["yx%d" % c], sem="o%d" % (3 + c), x=2.0)

    if not ORDER:
        ORDER.extend(schedule(ops, ["V", "S", "P", "G", "Y", "N"]))
    count = {}
    done = {}
    seen = {}
    for i in ORDER:
        o = ops[i]
        e = o["e"]
        if e != "N":
            for d, raw in sorted(o["dep"].items()):
                od = ops[d]
                if od["e"] == e == "P" and not raw:
                    continue
                if d not in done:
                    continue
                sm, val = done[d]
                if seen.get((e, sm), 0) < val:
                    seen[(e, sm)] = val
                    queue[e].wait_ge(T.sem[sm], val)
            ins = o["fn"]()
        if o["sem"] is None:
            count[e] = count.get(e, 0) + 1
            ins.then_inc(T.sem[e], 1)
            done[i] = (e, count[e])
        elif o["inc"] is None:
            ins.then_inc(T.sem[o["sem"]], 16)
            done[i] = (o["sem"], 16)
            count[o["sem"]] = 16
        elif e == "G":
            count["sent"] = count.get("sent", 0) + o["inc"]
        else:
            done[i] = (o["sem"], o["inc"])
            count[o["sem"]] = o["inc"]
    for sm in sorted(count):
        if seen.get(("G", sm), 0) < count[sm]:
            g.wait_ge(T.sem[sm], count[sm])
